import numpy as np
import ml_dtypes


def mxq(x, axis, fmt="e4m3"):
    dtype, down = {"e4m3": (ml_dtypes.float8_e4m3fn, 7), "e5m2": (ml_dtypes.float8_e5m2, 14)}[fmt]
    v = np.moveaxis(np.asarray(x, np.float32).astype(ml_dtypes.bfloat16).astype(np.float64), axis, -1)
    blocks = v.reshape(v.shape[:-1] + (-1, 32))
    amax = np.abs(blocks).max(-1, keepdims=True)
    byte = np.maximum(np.where(amax > 0, np.frexp(amax)[1] - 1 + 127, 0) - down, 1)
    scale = np.exp2(byte - 127.0)
    codes = (blocks / scale).astype(np.float32).astype(dtype).astype(np.float64)
    return np.moveaxis((codes * scale).reshape(v.shape), -1, axis)


WIDE = False


def mx_kscale(k):
    if not WIDE:
        return np.ones(k)
    levels = np.array([10, -10, 5, -5, 0])
    if k % 512:
        return np.exp2(np.random.permutation(np.resize(levels, k // 32))).repeat(32)
    a = np.empty((k // 512, 16))
    for p in range(k // 512):
        a[p, :8] = np.random.permutation(np.resize(levels, 8))
        for g in range(8):
            far = levels[np.abs(levels - a[p, g]) >= 10]
            a[p, g + 8] = far[np.random.randint(len(far))]
    return np.exp2(a.ravel()).repeat(32)


def f64(x):
    return np.asarray(x).astype(np.float64)


def striped8(idx):
    return np.concatenate([v.reshape(-1, 16).T for v in idx]).astype(np.uint16)


def unstriped8(offs):
    return np.stack([offs[16 * g:16 * g + 16].T.reshape(-1) for g in range(8)]).astype(np.int64)


E2M1 = np.array([0.0, 0.5, 1.0, 1.5, 2.0, 3.0, 4.0, 6.0, -0.0, -0.5, -1.0, -1.5, -2.0, -3.0, -4.0, -6.0])


def pack_weight(w, fmt):
    k, n = w.shape
    w = f64(np.asarray(w, np.float32).astype(ml_dtypes.bfloat16)).reshape(k // 32, 32, n)
    amax = np.abs(w).max(1)
    if fmt == "e4m3":
        byte = np.frexp(amax)[1] - 1 + 127 - 7
    else:
        mant, ex = np.frexp(amax / 6.0)
        byte = np.where(mant > 0.5, ex, ex - 1) + 127
    byte = np.clip(np.where(amax > 0, byte, 1), 1, 254)
    scaled = (w * np.exp2(127.0 - byte)[:, None, :]).reshape(k, n).astype(np.float32)
    by_word = np.ascontiguousarray(scaled.reshape(k // 512, 128, 4, n).transpose(0, 1, 3, 2))
    if fmt == "e4m3":
        words = by_word.astype(ml_dtypes.float8_e4m3fn).view(np.uint8)
    else:
        c = by_word.astype(ml_dtypes.float4_e2m1fn).view(np.uint8) & 0xF
        words = (c[..., 0::2] | (c[..., 1::2] << 4)).reshape(k // 512, 128, 2 * n)
    return np.ascontiguousarray(words), np.ascontiguousarray(byte.astype(np.uint8).reshape(k // 512, 16, n))


def unpack_weight(words, scales, fmt):
    g, _, n = scales.shape
    words = np.ascontiguousarray(words).reshape(g, 128, n, -1)
    if fmt == "e4m3":
        vals = words.view(ml_dtypes.float8_e4m3fn).astype(np.float64)
    else:
        nib = np.empty((g, 128, n, 4), np.uint8)
        nib[..., 0::2] = words & 0xF
        nib[..., 1::2] = words >> 4
        vals = E2M1[nib]
    vals = vals * np.repeat(np.exp2(scales.astype(np.float64) - 127.0), 8, axis=1)[..., None]
    return vals.transpose(0, 1, 3, 2).reshape(g * 512, n)


K, M, T, S = 512, 256, 2048, 1024


def setup_inputs():
    n = np.random.standard_normal
    s = mx_kscale(K)[:, None]
    w = n((K, M)) / np.sqrt(K) / s
    w4 = pack_weight(w, "e2m1")
    rest = w - unpack_weight(*w4, "e2m1")
    p_r8 = pack_weight(rest, "e4m3")
    return {
        "xT": (n((K, T)) * s).astype(np.float32),
        "w4_words": w4[0],
        "w4_scales": w4[1],
        "r8_words": p_r8[0],
        "r8_scales": p_r8[1],
        "wgt": np.repeat(np.random.uniform(0.5, 2.0, (8, S)), 16, axis=0).astype(np.float32),
        "offs": striped8(np.stack([np.random.permutation(T)[:S] for _ in range(8)])),
    }


def reference(xT, w4_words, w4_scales, r8_words, r8_scales, wgt, offs):
    idx = unstriped8(offs)
    group = np.arange(K) % 512 // 64
    xg = f64(wgt)[np.arange(K) // 4 % 128] * f64(xT)[np.arange(K)[:, None], idx[group]]
    xT_ = mxq(xg, 0, "e4m3")
    w4_ = unpack_weight(w4_words, w4_scales, "e2m1")
    r8_ = unpack_weight(r8_words, r8_scales, "e4m3")
    y = w4_.T @ xT_ + r8_.T @ xT_
    return y

@@ -1,0 +1,140 @@
+from contextlib import ExitStack
+
+import concourse.mybir as mybir
+from concourse.masks import make_identity
+
+K, M, T, S = 512, 256, 2048, 1024
+FLOPS = 2 * 2 * K * M * S
+
+F32 = mybir.dt.float32
+BF16 = mybir.dt.bfloat16
+I32 = mybir.dt.int32
+U32 = mybir.dt.uint32
+U16 = mybir.dt.uint16
+U8 = mybir.dt.uint8
+FP8X4 = mybir.dt.float8_e4m3fn_x4
+FP4X4 = mybir.dt.float4_e2m1fn_x4
+MULT = mybir.AluOpType.mult
+
+P = 128
+PACK = 4
+
+
+def tile_list_heads_none_kernel(
+    tc, xT, w4_words, w4_scales, r8_words, r8_scales, wgt, offs, out
+):
+    nc = tc.nc
+    planes = xT.rearrange("(p i) t -> i p t", i=PACK)
+
+    with ExitStack() as ctx:
+        lists = ctx.enter_context(tc.tile_pool(name="lists", bufs=1))
+        keep = ctx.enter_context(tc.tile_pool(name="keep", bufs=1))
+        psum = ctx.enter_context(tc.psum_pool(name="psum", bufs=1))
+
+        offsets = lists.tile([P, S // 16], U16, name="offsets")
+        weight = keep.tile([P, S], F32, name="weight", align_bytes=64)
+        xs = [keep.tile([P, T], F32, name=f"x{i}", align_bytes=64) for i in range(PACK)]
+        w4 = keep.tile([P, 2 * M], U8, name="w4", align_bytes=64)
+        r8 = keep.tile([P, M], U32, name="r8", align_bytes=64)
+        w4s = keep.tile([P, M], U8, name="w4s", align_bytes=64)
+        r8s = keep.tile([P, M], U8, name="r8s", align_bytes=64)
+        g = [keep.tile([P, 2, S], F32, name=f"g{h}", align_bytes=64) for h in range(2)]
+        xb = keep.tile([P, S, PACK], BF16, name="xb", align_bytes=64)
+        codes = keep.tile([P, S], U32, name="codes", align_bytes=64)
+        scales = keep.tile([P, S], U8, name="scales", align_bytes=64)
+
+        nc.vector.memset(r8s[:].bitcast(I32), 0)
+        nc.vector.memset(w4s[:].bitcast(I32), 0)
+
+        def load_scales(engine, tile, src, q):
+            engine.dma_start(tile[32 * q : 32 * q + 4, :].bitcast(I32), src[0, 4 * q : 4 * q + 4, :].bitcast(I32))
+
+        for q in range(4):
+            load_scales(nc.gpsimd, r8s, r8_scales, q)
+
+        nc.sync.dma_start(offsets[:], offs)
+        nc.sync.dma_start(weight[:, 0:256], wgt[:, 0:256])
+        nc.sync.dma_start(xs[0][:], planes[0])
+        nc.sync.dma_start(weight[:, 256:1024], wgt[:, 256:1024])
+        nc.sync.dma_start(xs[1][:], planes[1])
+        for q in range(3):
+            load_scales(nc.sync, w4s, w4_scales, q)
+        nc.sync.dma_start(xs[2][:], planes[2])
+        load_scales(nc.sync, w4s, w4_scales, 3)
+        nc.sync.dma_start(xs[3][:], planes[3])
+        nc.sync.dma_start(w4[:].bitcast(I32), w4_words[0].bitcast(I32))
+        nc.sync.dma_start(r8[:].bitcast(I32), r8_words[0].rearrange("p n t -> p (n t)").bitcast(I32))
+
+        ident = keep.tile([P, P], F32, name="ident", align_bytes=64)
+        make_identity(nc, ident[:])
+        warm = psum.tile([P, 256], F32, name="acc768_1")
+
+        def warm_up(src):
+            nc.tensor.transpose(warm[:, 0:128], src, ident[:])
+
+        def gather(i, a, b):
+            nc.vector.tensor_tensor(
+                g[i // 2][:, i % 2, a:b], xs[i][:].indirect(offsets[:, a // 16 : b // 16]), weight[:, a:b], MULT
+            )
+
+        def interleave(copy, h, a, b):
+            copy(xb[:, a:b, 2 * h : 2 * h + 2], g[h][:, :, a:b].rearrange("p t n -> p n t"))
+
+        for i in range(3):
+            if i == 0:
+                gather(i, 0, 256)
+                gather(i, 256, 512)
+            else:
+                gather(i, 0, 512)
+            gather(i, 512, 1024)
+            if i == 1:
+                interleave(nc.scalar.copy, 0, 0, 512)
+                interleave(nc.scalar.copy, 0, 512, 1024)
+
+        for a in range(512, 1024, 128):
+            for turn in range(2):
+                warm_up(g[1][:, 0, a : a + 128])
+
+        chunks = ((0, 256, nc.scalar.copy), (256, 256, nc.scalar.copy), (512, 256, nc.scalar.copy), (768, 256, nc.vector.tensor_copy))
+        for a, w, copy in chunks:
+            gather(3, a, a + w)
+            if a < 512:
+                for b in range(a, a + 256, 128):
+                    for turn in range(2):
+                        warm_up(g[1][:, 1, b : b + 128])
+            for b in range(a, a + w, 128 if a == 0 else w):
+                interleave(copy, 1, b, b + (128 if a == 0 else w))
+            for b in range(a, a + w, 128):
+                nc.vector.quantize_mx(
+                    out=codes[:, b : b + 128].bitcast(FP8X4),
+                    scales=scales[:, b : b + 128],
+                    in_=xb[:, b : b + 128, :].rearrange("p n t -> p (n t)"),
+                )
+            for m in range(2):
+                acc = psum.tile([P, w], F32, name=f"acc{a}_{m}")
+                for b in range(0, w, 128):
+                    cols = slice(a + b, a + b + 128)
+                    nc.tensor.matmul_mx(
+                        out=acc[:, b : b + 128],
+                        lhsT=w4[:, 256 * m : 256 * m + 256].bitcast(FP4X4),
+                        lhsT_scale=w4s[:, 128 * m : 128 * m + 128],
+                        rhs=codes[:, cols].bitcast(FP8X4),
+                        rhs_scale=scales[:, cols],
+                        start=True,
+                        stop=False,
+                    )
+                    nc.tensor.matmul_mx(
+                        out=acc[:, b : b + 128],
+                        lhsT=r8[:, 128 * m : 128 * m + 128].bitcast(FP8X4),
+                        lhsT_scale=r8s[:, 128 * m : 128 * m + 128],
+                        rhs=codes[:, cols].bitcast(FP8X4),
+                        rhs_scale=scales[:, cols],
+                        start=False,
+                        stop=True,
+                    )
+                res = keep.tile([P, w], F32, name=f"res{a}_{m}", align_bytes=64)
+                if m == 0 or a < 512:
+                    nc.scalar.copy(res[:], acc[:])
+                else:
+                    nc.vector.tensor_copy(res[:], acc[:])
+                nc.sync.dma_start(out[128 * m : 128 * m + 128, a : a + w], res[:])

@@ -52,18 +52,29 @@ def tile_list_heads_none_kernel(
         for q in range(4):
             load_scales(nc.gpsimd, r8s, r8_scales, q)
 
-        nc.sync.dma_start(offsets[:], offs)
-        nc.sync.dma_start(weight[:, 0:256], wgt[:, 0:256])
+        rows = keep.tile([P, 64], F32, name="rows", align_bytes=64)
+        turned = keep.tile([P, 64], F32, name="turned", align_bytes=64)
+        spread = keep.tile([P, S], F32, name="spread", align_bytes=64)
+        nc.sync.dma_start(rows[:], wgt.rearrange("(g r) (b e) -> r g b e", r=16, e=64)[0])
         nc.sync.dma_start(xs[0][:], planes[0])
-        nc.sync.dma_start(weight[:, 256:1024], wgt[:, 256:1024])
-        nc.sync.dma_start(xs[1][:], planes[1])
-        for q in range(3):
-            load_scales(nc.sync, w4s, w4_scales, q)
-        nc.sync.dma_start(xs[2][:], planes[2])
-        load_scales(nc.sync, w4s, w4_scales, 3)
-        nc.sync.dma_start(xs[3][:], planes[3])
+        nc.sync.dma_start(offsets[:], offs)
+        for i in range(1, PACK):
+            nc.sync.dma_start(xs[i][:], planes[i])
         nc.sync.dma_start(w4[:].bitcast(I32), w4_words[0].bitcast(I32))
         nc.sync.dma_start(r8[:].bitcast(I32), r8_words[0].rearrange("p n t -> p (n t)").bitcast(I32))
+        for q in range(4):
+            load_scales(nc.sync, w4s, w4_scales, q)
+
+        for a in (0, 32):
+            nc.vector.transpose(turned[:, a : a + 32], rows[:, a : a + 32])
+        by_block = turned[:].rearrange("p (c b) -> p b c", b=16)
+        for a in (0, 512):
+            nc.vector.tensor_copy(
+                spread[:, a : a + 512].rearrange("p (b c r) -> p b c r", c=4, r=16),
+                by_block[:, a // 64 : a // 64 + 8, :].unsqueeze(3).broadcast_to([P, 8, 4, 16]),
+            )
+        for a in (0, 512):
+            nc.vector.transpose(weight[:, a : a + 512], spread[:, a : a + 512])
 
         ident = keep.tile([P, P], F32, name="ident", align_bytes=64)
         make_identity(nc, ident[:])
@@ -81,11 +92,7 @@ def tile_list_heads_none_kernel(
             copy(xb[:, a:b, 2 * h : 2 * h + 2], g[h][:, :, a:b].rearrange("p t n -> p n t"))
 
         for i in range(3):
-            if i == 0:
-                gather(i, 0, 256)
-                gather(i, 256, 512)
-            else:
-                gather(i, 0, 512)
+            gather(i, 0, 512)
             gather(i, 512, 1024)
             if i == 1:
                 interleave(nc.scalar.copy, 0, 0, 512)

@@ -1,7 +1,6 @@
 from contextlib import ExitStack
 
 import concourse.mybir as mybir
-from concourse.masks import make_identity
 
 K, M, T, S = 512, 256, 2048, 1024
 FLOPS = 2 * 2 * K * M * S
@@ -76,13 +75,6 @@ def tile_list_heads_none_kernel(
         for a in (0, 512):
             nc.vector.transpose(weight[:, a : a + 512], spread[:, a : a + 512])
 
-        ident = keep.tile([P, P], F32, name="ident", align_bytes=64)
-        make_identity(nc, ident[:])
-        warm = psum.tile([P, 256], F32, name="acc768_1")
-
-        def warm_up(src):
-            nc.tensor.transpose(warm[:, 0:128], src, ident[:])
-
         def gather(i, a, b):
             nc.vector.tensor_tensor(
                 g[i // 2][:, i % 2, a:b], xs[i][:].indirect(offsets[:, a // 16 : b // 16]), weight[:, a:b], MULT
@@ -98,17 +90,9 @@ def tile_list_heads_none_kernel(
                 interleave(nc.scalar.copy, 0, 0, 512)
                 interleave(nc.scalar.copy, 0, 512, 1024)
 
-        for a in range(512, 1024, 128):
-            for turn in range(2):
-                warm_up(g[1][:, 0, a : a + 128])
-
         chunks = ((0, 256, nc.scalar.copy), (256, 256, nc.scalar.copy), (512, 256, nc.scalar.copy), (768, 256, nc.vector.tensor_copy))
         for a, w, copy in chunks:
             gather(3, a, a + w)
-            if a < 512:
-                for b in range(a, a + 256, 128):
-                    for turn in range(2):
-                        warm_up(g[1][:, 1, b : b + 128])
             for b in range(a, a + w, 128 if a == 0 else w):
                 interleave(copy, 1, b, b + (128 if a == 0 else w))
             for b in range(a, a + w, 128):

@@ -17,6 +17,10 @@ MULT = mybir.AluOpType.mult
 
 P = 128
 PACK = 4
+CHUNK = 128
+CHUNKS = S // CHUNK
+ON_VECTOR = (0, 5, 6, 7,)
+GATHER_STARTS = (0, 1, 2, 3, 4, 5, 6, 7,)
 
 
 def tile_list_heads_none_kernel(
@@ -24,6 +28,7 @@ def tile_list_heads_none_kernel(
 ):
     nc = tc.nc
     planes = xT.rearrange("(p i) t -> i p t", i=PACK)
+    out_halves = out.rearrange("(m p) j -> p m j", p=P)
 
     with ExitStack() as ctx:
         lists = ctx.enter_context(tc.tile_pool(name="lists", bufs=1))
@@ -37,7 +42,8 @@ def tile_list_heads_none_kernel(
         r8 = keep.tile([P, M], U32, name="r8", align_bytes=64)
         w4s = keep.tile([P, M], U8, name="w4s", align_bytes=64)
         r8s = keep.tile([P, M], U8, name="r8s", align_bytes=64)
-        g = [keep.tile([P, 2, S], F32, name=f"g{h}", align_bytes=64) for h in range(2)]
+        early = keep.tile([P, 2, S], F32, name="early", align_bytes=64)
+        late = keep.tile([P, 2, S], F32, name="late", align_bytes=64)
         xb = keep.tile([P, S, PACK], BF16, name="xb", align_bytes=64)
         codes = keep.tile([P, S], U32, name="codes", align_bytes=64)
         scales = keep.tile([P, S], U8, name="scales", align_bytes=64)
@@ -75,57 +81,66 @@ def tile_list_heads_none_kernel(
         for a in (0, 512):
             nc.vector.transpose(weight[:, a : a + 512], spread[:, a : a + 512])
 
-        def gather(i, a, b):
-            nc.vector.tensor_tensor(
-                g[i // 2][:, i % 2, a:b], xs[i][:].indirect(offsets[:, a // 16 : b // 16]), weight[:, a:b], MULT
+
+        def gather(dst, i, a, b):
+            nc.vector.tensor_tensor(dst, xs[i][:].indirect(offsets[:, a // 16 : b // 16]), weight[:, a:b], MULT)
+
+        def interleave(copy, src, h, a, b):
+            copy(xb[:, a:b, 2 * h : 2 * h + 2], src.rearrange("p t n -> p n t"))
+
+        for a, b in ((0, 512), (512, 1024)):
+            gather(early[:, 0, a:b], 0, a, b)
+        for a, b in ((0, 512), (512, 1024)):
+            gather(early[:, 1, a:b], 1, a, b)
+            interleave(nc.scalar.copy, early[:, :, a:b], 0, a, b)
+        gather(late[:, 0, :], 2, 0, S)
+        gather_ends = dict(zip(GATHER_STARTS, GATHER_STARTS[1:] + (CHUNKS,)))
+
+        def multiply(acc, m, cols):
+            nc.tensor.matmul_mx(
+                out=acc,
+                lhsT=w4[:, 256 * m : 256 * m + 256].bitcast(FP4X4),
+                lhsT_scale=w4s[:, 128 * m : 128 * m + 128],
+                rhs=codes[:, cols].bitcast(FP8X4),
+                rhs_scale=scales[:, cols],
+                start=True,
+                stop=False,
+            )
+            nc.tensor.matmul_mx(
+                out=acc,
+                lhsT=r8[:, 128 * m : 128 * m + 128].bitcast(FP8X4),
+                lhsT_scale=r8s[:, 128 * m : 128 * m + 128],
+                rhs=codes[:, cols].bitcast(FP8X4),
+                rhs_scale=scales[:, cols],
+                start=False,
+                stop=True,
             )
 
-        def interleave(copy, h, a, b):
-            copy(xb[:, a:b, 2 * h : 2 * h + 2], g[h][:, :, a:b].rearrange("p t n -> p n t"))
-
-        for i in range(3):
-            gather(i, 0, 512)
-            gather(i, 512, 1024)
-            if i == 1:
-                interleave(nc.scalar.copy, 0, 0, 512)
-                interleave(nc.scalar.copy, 0, 512, 1024)
-
-        chunks = ((0, 256, nc.scalar.copy), (256, 256, nc.scalar.copy), (512, 256, nc.scalar.copy), (768, 256, nc.vector.tensor_copy))
-        for a, w, copy in chunks:
-            gather(3, a, a + w)
-            for b in range(a, a + w, 128 if a == 0 else w):
-                interleave(copy, 1, b, b + (128 if a == 0 else w))
-            for b in range(a, a + w, 128):
+        groups = ((0, 2, False), (2, 2, False), (4, 1, False), (5, 1, False), (6, 1, True), (7, 1, True))
+        for first, n, split in groups:
+            w = n * CHUNK
+            if split:
+                banks = [psum.tile([P, w], F32, name=f"acc{first}_{m}")[:] for m in range(2)]
+            else:
+                both = psum.tile([P, 2, w], F32, name=f"acc{first}")
+                banks = [both[:, m, :] for m in range(2)]
+            res = keep.tile([P, 2, w], F32, name=f"res{first}", align_bytes=64)
+            for c in range(first, first + n):
+                cols = slice(CHUNK * c, CHUNK * (c + 1))
+                if c in gather_ends:
+                    gather(late[:, 1, cols.start : CHUNK * gather_ends[c]], 3, cols.start, CHUNK * gather_ends[c])
+                copy = nc.vector.tensor_copy if c in ON_VECTOR else nc.scalar.copy
+                interleave(copy, late[:, :, cols], 1, cols.start, cols.stop)
                 nc.vector.quantize_mx(
-                    out=codes[:, b : b + 128].bitcast(FP8X4),
-                    scales=scales[:, b : b + 128],
-                    in_=xb[:, b : b + 128, :].rearrange("p n t -> p (n t)"),
+                    out=codes[:, cols].bitcast(FP8X4),
+                    scales=scales[:, cols],
+                    in_=xb[:, cols, :].rearrange("p n t -> p (n t)"),
                 )
-            for m in range(2):
-                acc = psum.tile([P, w], F32, name=f"acc{a}_{m}")
-                for b in range(0, w, 128):
-                    cols = slice(a + b, a + b + 128)
-                    nc.tensor.matmul_mx(
-                        out=acc[:, b : b + 128],
-                        lhsT=w4[:, 256 * m : 256 * m + 256].bitcast(FP4X4),
-                        lhsT_scale=w4s[:, 128 * m : 128 * m + 128],
-                        rhs=codes[:, cols].bitcast(FP8X4),
-                        rhs_scale=scales[:, cols],
-                        start=True,
-                        stop=False,
-                    )
-                    nc.tensor.matmul_mx(
-                        out=acc[:, b : b + 128],
-                        lhsT=r8[:, 128 * m : 128 * m + 128].bitcast(FP8X4),
-                        lhsT_scale=r8s[:, 128 * m : 128 * m + 128],
-                        rhs=codes[:, cols].bitcast(FP8X4),
-                        rhs_scale=scales[:, cols],
-                        start=False,
-                        stop=True,
-                    )
-                res = keep.tile([P, w], F32, name=f"res{a}_{m}", align_bytes=64)
-                if m == 0 or a < 512:
-                    nc.scalar.copy(res[:], acc[:])
-                else:
-                    nc.vector.tensor_copy(res[:], acc[:])
-                nc.sync.dma_start(out[128 * m : 128 * m + 128, a : a + w], res[:])
+                for m in range(2):
+                    multiply(banks[m][:, CHUNK * (c - first) : CHUNK * (c - first + 1)], m, cols)
+            if split:
+                nc.scalar.copy(res[:, 0, :], banks[0])
+                nc.vector.tensor_copy(res[:, 1, :], banks[1])
+            else:
+                nc.scalar.copy(res[:], both[:])
+            nc.sync.dma_start(out_halves[:, :, CHUNK * first : CHUNK * first + w], res[:])

@@ -88,8 +88,7 @@ def tile_list_heads_none_kernel(
         def interleave(copy, src, h, a, b):
             copy(xb[:, a:b, 2 * h : 2 * h + 2], src.rearrange("p t n -> p n t"))
 
-        for a, b in ((0, 512), (512, 1024)):
-            gather(early[:, 0, a:b], 0, a, b)
+        gather(early[:, 0, :], 0, 0, S)
         for a, b in ((0, 512), (512, 1024)):
             gather(early[:, 1, a:b], 1, a, b)
             interleave(nc.scalar.copy, early[:, :, a:b], 0, a, b)
@@ -116,11 +115,11 @@ def tile_list_heads_none_kernel(
                 stop=True,
             )
 
-        groups = ((0, 2, False), (2, 2, False), (4, 1, False), (5, 1, False), (6, 1, True), (7, 1, True))
+        groups = tuple((c, 1, c >= 6) for c in range(CHUNKS))
         for first, n, split in groups:
             w = n * CHUNK
             if split:
-                banks = [psum.tile([P, w], F32, name=f"acc{first}_{m}")[:] for m in range(2)]
+                banks = [psum.tile([P, w], F32, name=f"acc{first - 6 * m}")[:] for m in range(2)]
             else:
                 both = psum.tile([P, 2, w], F32, name=f"acc{first}")
                 banks = [both[:, m, :] for m in range(2)]
@@ -143,4 +142,8 @@ def tile_list_heads_none_kernel(
                 nc.vector.tensor_copy(res[:, 1, :], banks[1])
             else:
                 nc.scalar.copy(res[:], both[:])
-            nc.sync.dma_start(out_halves[:, :, CHUNK * first : CHUNK * first + w], res[:])
+            if first == CHUNKS - 1:
+                for m in range(2):
+                    nc.sync.dma_start(out_halves[:, m, CHUNK * first : CHUNK * first + w], res[:, m, :])
+            else:
+                nc.sync.dma_start(out_halves[:, :, CHUNK * first : CHUNK * first + w], res[:])

@@ -19,8 +19,7 @@ P = 128
 PACK = 4
 CHUNK = 128
 CHUNKS = S // CHUNK
-ON_VECTOR = (0, 5, 6, 7,)
-GATHER_STARTS = (0, 1, 2, 3, 4, 5, 6, 7,)
+ON_VECTOR = (0, 6, 7,)
 
 
 def tile_list_heads_none_kernel(
@@ -43,7 +42,8 @@ def tile_list_heads_none_kernel(
         w4s = keep.tile([P, M], U8, name="w4s", align_bytes=64)
         r8s = keep.tile([P, M], U8, name="r8s", align_bytes=64)
         early = keep.tile([P, 2, S], F32, name="early", align_bytes=64)
-        late = keep.tile([P, 2, S], F32, name="late", align_bytes=64)
+        late = keep.tile([P, 2, 5 * CHUNK], F32, name="late", align_bytes=64)
+        ends = keep.tile([P, 4, CHUNK], F32, name="ends", align_bytes=64)
         xb = keep.tile([P, S, PACK], BF16, name="xb", align_bytes=64)
         codes = keep.tile([P, S], U32, name="codes", align_bytes=64)
         scales = keep.tile([P, S], U8, name="scales", align_bytes=64)
@@ -60,7 +60,7 @@ def tile_list_heads_none_kernel(
         rows = keep.tile([P, 64], F32, name="rows", align_bytes=64)
         turned = keep.tile([P, 64], F32, name="turned", align_bytes=64)
         spread = keep.tile([P, S], F32, name="spread", align_bytes=64)
-        nc.sync.dma_start(rows[:], wgt.rearrange("(g r) (b e) -> r g b e", r=16, e=64)[0])
+        nc.sync.dma_start(rows[:], wgt.rearrange("p (h e) -> (p h) e", e=512)[0:256:17])
         nc.sync.dma_start(xs[0][:], planes[0])
         nc.sync.dma_start(offsets[:], offs)
         for i in range(1, PACK):
@@ -73,8 +73,8 @@ def tile_list_heads_none_kernel(
         for a in (0, 32):
             nc.vector.transpose(turned[:, a : a + 32], rows[:, a : a + 32])
         by_block = turned[:].rearrange("p (c b) -> p b c", b=16)
-        for a in (0, 512):
-            nc.vector.tensor_copy(
+        for a, copy in ((0, nc.vector.tensor_copy), (512, nc.scalar.copy)):
+            copy(
                 spread[:, a : a + 512].rearrange("p (b c r) -> p b c r", c=4, r=16),
                 by_block[:, a // 64 : a // 64 + 8, :].unsqueeze(3).broadcast_to([P, 8, 4, 16]),
             )
@@ -92,8 +92,16 @@ def tile_list_heads_none_kernel(
         for a, b in ((0, 512), (512, 1024)):
             gather(early[:, 1, a:b], 1, a, b)
             interleave(nc.scalar.copy, early[:, :, a:b], 0, a, b)
-        gather(late[:, 0, :], 2, 0, S)
-        gather_ends = dict(zip(GATHER_STARTS, GATHER_STARTS[1:] + (CHUNKS,)))
+        gather(ends[:, 0, :], 2, 0, CHUNK)
+        gather(late[:, 0, :], 2, CHUNK, 6 * CHUNK)
+
+        def pair(c):
+            if c == 0:
+                return ends[:, 0:2, :]
+            if c < 6:
+                return late[:, :, CHUNK * (c - 1) : CHUNK * c]
+            return ends[:, c - 6 : 4 : 2, :]
+
 
         def multiply(acc, m, cols):
             nc.tensor.matmul_mx(
@@ -115,21 +123,22 @@ def tile_list_heads_none_kernel(
                 stop=True,
             )
 
-        groups = tuple((c, 1, c >= 6) for c in range(CHUNKS))
+        groups = tuple((c, 1, c in (0, 6, 7)) for c in range(CHUNKS))
         for first, n, split in groups:
             w = n * CHUNK
             if split:
-                banks = [psum.tile([P, w], F32, name=f"acc{first - 6 * m}")[:] for m in range(2)]
+                banks = [psum.tile([P, w], F32, name=f"acc{b}")[:] for b in {0: (0, 7), 6: (6, 0), 7: (7, 1)}[first]]
             else:
                 both = psum.tile([P, 2, w], F32, name=f"acc{first}")
                 banks = [both[:, m, :] for m in range(2)]
             res = keep.tile([P, 2, w], F32, name=f"res{first}", align_bytes=64)
             for c in range(first, first + n):
                 cols = slice(CHUNK * c, CHUNK * (c + 1))
-                if c in gather_ends:
-                    gather(late[:, 1, cols.start : CHUNK * gather_ends[c]], 3, cols.start, CHUNK * gather_ends[c])
+                if c == 6:
+                    gather(ends[:, 0:2, :].rearrange("p r n -> p (r n)"), 2, 6 * CHUNK, S)
+                gather(pair(c)[:, 1, :], 3, cols.start, cols.stop)
                 copy = nc.vector.tensor_copy if c in ON_VECTOR else nc.scalar.copy
-                interleave(copy, late[:, :, cols], 1, cols.start, cols.stop)
+                interleave(copy, pair(c), 1, cols.start, cols.stop)
                 nc.vector.quantize_mx(
                     out=codes[:, cols].bitcast(FP8X4),
                     scales=scales[:, cols],
@@ -139,10 +148,10 @@ def tile_list_heads_none_kernel(
                     multiply(banks[m][:, CHUNK * (c - first) : CHUNK * (c - first + 1)], m, cols)
             if split:
                 nc.scalar.copy(res[:, 0, :], banks[0])
-                nc.vector.tensor_copy(res[:, 1, :], banks[1])
+                (nc.vector.tensor_copy if first else nc.scalar.copy)(res[:, 1, :], banks[1])
             else:
                 nc.scalar.copy(res[:], both[:])
-            if first == CHUNKS - 1:
+            if first in (0, CHUNKS - 1):
                 for m in range(2):
                     nc.sync.dma_start(out_halves[:, m, CHUNK * first : CHUNK * first + w], res[:, m, :])
             else:

@@ -54,9 +54,6 @@ def tile_list_heads_none_kernel(
         def load_scales(engine, tile, src, q):
             engine.dma_start(tile[32 * q : 32 * q + 4, :].bitcast(I32), src[0, 4 * q : 4 * q + 4, :].bitcast(I32))
 
-        for q in range(4):
-            load_scales(nc.gpsimd, r8s, r8_scales, q)
-
         rows = keep.tile([P, 64], F32, name="rows", align_bytes=64)
         turned = keep.tile([P, 64], F32, name="turned", align_bytes=64)
         spread = keep.tile([P, S], F32, name="spread", align_bytes=64)
@@ -65,6 +62,8 @@ def tile_list_heads_none_kernel(
         nc.sync.dma_start(offsets[:], offs)
         for i in range(1, PACK):
             nc.sync.dma_start(xs[i][:], planes[i])
+            for q in ((0, 1), (2,), (3,))[i - 1]:
+                load_scales(nc.sync, r8s, r8_scales, q)
         nc.sync.dma_start(w4[:].bitcast(I32), w4_words[0].bitcast(I32))
         nc.sync.dma_start(r8[:].bitcast(I32), r8_words[0].rearrange("p n t -> p (n t)").bitcast(I32))
         for q in range(4):
@@ -136,7 +135,10 @@ def tile_list_heads_none_kernel(
                 cols = slice(CHUNK * c, CHUNK * (c + 1))
                 if c == 6:
                     gather(ends[:, 0:2, :].rearrange("p r n -> p (r n)"), 2, 6 * CHUNK, S)
-                gather(pair(c)[:, 1, :], 3, cols.start, cols.stop)
+                if c == 6:
+                    gather(ends[:, 2:4, :].rearrange("p r n -> p (r n)"), 3, 6 * CHUNK, S)
+                elif c < 6:
+                    gather(pair(c)[:, 1, :], 3, cols.start, cols.stop)
                 copy = nc.vector.tensor_copy if c in ON_VECTOR else nc.scalar.copy
                 interleave(copy, pair(c), 1, cols.start, cols.stop)
                 nc.vector.quantize_mx(

@@ -19,6 +19,7 @@ P = 128
 PACK = 4
 CHUNK = 128
 CHUNKS = S // CHUNK
+HOLDER = 2
 ON_VECTOR = (0, 6, 7,)
 
 
@@ -42,7 +43,8 @@ def tile_list_heads_none_kernel(
         w4s = keep.tile([P, M], U8, name="w4s", align_bytes=64)
         r8s = keep.tile([P, M], U8, name="r8s", align_bytes=64)
         early = keep.tile([P, 2, S], F32, name="early", align_bytes=64)
-        late = keep.tile([P, 2, 5 * CHUNK], F32, name="late", align_bytes=64)
+        before = keep.tile([P, 2, HOLDER * CHUNK], F32, name="before", align_bytes=64)
+        after = keep.tile([P, 2, (5 - HOLDER) * CHUNK], F32, name="after", align_bytes=64)
         ends = keep.tile([P, 4, CHUNK], F32, name="ends", align_bytes=64)
         xb = keep.tile([P, S, PACK], BF16, name="xb", align_bytes=64)
         codes = keep.tile([P, S], U32, name="codes", align_bytes=64)
@@ -91,14 +93,17 @@ def tile_list_heads_none_kernel(
         for a, b in ((0, 512), (512, 1024)):
             gather(early[:, 1, a:b], 1, a, b)
             interleave(nc.scalar.copy, early[:, :, a:b], 0, a, b)
-        gather(ends[:, 0, :], 2, 0, CHUNK)
-        gather(late[:, 0, :], 2, CHUNK, 6 * CHUNK)
+        gather(before[:, 0, :], 2, 0, HOLDER * CHUNK)
+        gather(ends[:, 1, :], 2, HOLDER * CHUNK, (HOLDER + 1) * CHUNK)
+        gather(after[:, 0, :], 2, (HOLDER + 1) * CHUNK, 6 * CHUNK)
 
         def pair(c):
-            if c == 0:
-                return ends[:, 0:2, :]
+            if c < HOLDER:
+                return before[:, :, CHUNK * c : CHUNK * (c + 1)]
+            if c == HOLDER:
+                return ends[:, 1:3, :]
             if c < 6:
-                return late[:, :, CHUNK * (c - 1) : CHUNK * c]
+                return after[:, :, CHUNK * (c - HOLDER - 1) : CHUNK * (c - HOLDER)]
             return ends[:, c - 6 : 4 : 2, :]
 
 

@@ -107,16 +107,19 @@ def tile_list_heads_none_kernel(
             return ends[:, c - 6 : 4 : 2, :]
 
 
-        def multiply(acc, m, cols):
-            nc.tensor.matmul_mx(
-                out=acc,
-                lhsT=w4[:, 256 * m : 256 * m + 256].bitcast(FP4X4),
-                lhsT_scale=w4s[:, 128 * m : 128 * m + 128],
-                rhs=codes[:, cols].bitcast(FP8X4),
-                rhs_scale=scales[:, cols],
-                start=True,
-                stop=False,
-            )
+        def multiply(acc, m, first, n):
+            for c in range(n):
+                cols = slice(CHUNK * (first + c), CHUNK * (first + c + 1))
+                nc.tensor.matmul_mx(
+                    out=acc[:, CHUNK * c : CHUNK * (c + 1)],
+                    lhsT=w4[:, 256 * m : 256 * m + 256].bitcast(FP4X4),
+                    lhsT_scale=w4s[:, 128 * m : 128 * m + 128],
+                    rhs=codes[:, cols].bitcast(FP8X4),
+                    rhs_scale=scales[:, cols],
+                    start=c == 0,
+                    stop=False,
+                )
+            cols = slice(CHUNK * first, CHUNK * (first + n))
             nc.tensor.matmul_mx(
                 out=acc,
                 lhsT=r8[:, 128 * m : 128 * m + 128].bitcast(FP8X4),
@@ -127,20 +130,20 @@ def tile_list_heads_none_kernel(
                 stop=True,
             )
 
-        groups = tuple((c, 1, c in (0, 6, 7)) for c in range(CHUNKS))
-        for first, n, split in groups:
+        groups = ((0, 1, (0, 1)), (1, 2, (2, 3)), (3, 1, (4,)), (4, 2, (5, 6)), (6, 1, (7, 0)), (7, 1, (1, 2)))
+        for first, n, names in groups:
             w = n * CHUNK
+            split = len(names) == 2
             if split:
-                banks = [psum.tile([P, w], F32, name=f"acc{b}")[:] for b in {0: (0, 7), 6: (6, 0), 7: (7, 1)}[first]]
+                banks = [psum.tile([P, w], F32, name=f"acc{b}")[:] for b in names]
             else:
-                both = psum.tile([P, 2, w], F32, name=f"acc{first}")
+                both = psum.tile([P, 2, w], F32, name=f"acc{names[0]}")
                 banks = [both[:, m, :] for m in range(2)]
             res = keep.tile([P, 2, w], F32, name=f"res{first}", align_bytes=64)
             for c in range(first, first + n):
                 cols = slice(CHUNK * c, CHUNK * (c + 1))
                 if c == 6:
                     gather(ends[:, 0:2, :].rearrange("p r n -> p (r n)"), 2, 6 * CHUNK, S)
-                if c == 6:
                     gather(ends[:, 2:4, :].rearrange("p r n -> p (r n)"), 3, 6 * CHUNK, S)
                 elif c < 6:
                     gather(pair(c)[:, 1, :], 3, cols.start, cols.stop)
@@ -151,14 +154,14 @@ def tile_list_heads_none_kernel(
                     scales=scales[:, cols],
                     in_=xb[:, cols, :].rearrange("p n t -> p (n t)"),
                 )
-                for m in range(2):
-                    multiply(banks[m][:, CHUNK * (c - first) : CHUNK * (c - first + 1)], m, cols)
+            for m in range(2):
+                multiply(banks[m], m, first, n)
             if split:
                 nc.scalar.copy(res[:, 0, :], banks[0])
-                (nc.vector.tensor_copy if first else nc.scalar.copy)(res[:, 1, :], banks[1])
+                (nc.vector.tensor_copy if first >= 6 else nc.scalar.copy)(res[:, 1, :], banks[1])
             else:
                 nc.scalar.copy(res[:], both[:])
-            if first in (0, CHUNKS - 1):
+            if split and first != 6:
                 for m in range(2):
                     nc.sync.dma_start(out_halves[:, m, CHUNK * first : CHUNK * first + w], res[:, m, :])
             else:

@@ -19,8 +19,10 @@ P = 128
 PACK = 4
 CHUNK = 128
 CHUNKS = S // CHUNK
+EARLY = 6
+RING = 3
 HOLDER = 2
-ON_VECTOR = (0, 6, 7,)
+LAG = 3
 
 
 def tile_list_heads_none_kernel(
@@ -43,9 +45,7 @@ def tile_list_heads_none_kernel(
         w4s = keep.tile([P, M], U8, name="w4s", align_bytes=64)
         r8s = keep.tile([P, M], U8, name="r8s", align_bytes=64)
         early = keep.tile([P, 2, S], F32, name="early", align_bytes=64)
-        before = keep.tile([P, 2, HOLDER * CHUNK], F32, name="before", align_bytes=64)
-        after = keep.tile([P, 2, (5 - HOLDER) * CHUNK], F32, name="after", align_bytes=64)
-        ends = keep.tile([P, 4, CHUNK], F32, name="ends", align_bytes=64)
+        late = keep.tile([P, EARLY + RING, CHUNK], F32, name="late", align_bytes=64)
         xb = keep.tile([P, S, PACK], BF16, name="xb", align_bytes=64)
         codes = keep.tile([P, S], U32, name="codes", align_bytes=64)
         scales = keep.tile([P, S], U8, name="scales", align_bytes=64)
@@ -62,14 +62,14 @@ def tile_list_heads_none_kernel(
         nc.sync.dma_start(rows[:], wgt.rearrange("p (h e) -> (p h) e", e=512)[0:256:17])
         nc.sync.dma_start(xs[0][:], planes[0])
         nc.sync.dma_start(offsets[:], offs)
+        for q in range(4):
+            load_scales(nc.gpsimd, w4s, w4_scales, q)
         for i in range(1, PACK):
             nc.sync.dma_start(xs[i][:], planes[i])
-            for q in ((0, 1), (2,), (3,))[i - 1]:
+            for q in ((0, 1), (2, 3), ())[i - 1]:
                 load_scales(nc.sync, r8s, r8_scales, q)
         nc.sync.dma_start(w4[:].bitcast(I32), w4_words[0].bitcast(I32))
         nc.sync.dma_start(r8[:].bitcast(I32), r8_words[0].rearrange("p n t -> p (n t)").bitcast(I32))
-        for q in range(4):
-            load_scales(nc.sync, w4s, w4_scales, q)
 
         for a in (0, 32):
             nc.vector.transpose(turned[:, a : a + 32], rows[:, a : a + 32])
@@ -93,33 +93,27 @@ def tile_list_heads_none_kernel(
         for a, b in ((0, 512), (512, 1024)):
             gather(early[:, 1, a:b], 1, a, b)
             interleave(nc.scalar.copy, early[:, :, a:b], 0, a, b)
-        gather(before[:, 0, :], 2, 0, HOLDER * CHUNK)
-        gather(ends[:, 1, :], 2, HOLDER * CHUNK, (HOLDER + 1) * CHUNK)
-        gather(after[:, 0, :], 2, (HOLDER + 1) * CHUNK, 6 * CHUNK)
+        gather(late[:, 0:EARLY, :].rearrange("p r n -> p (r n)"), 2, 0, EARLY * CHUNK)
 
-        def pair(c):
-            if c < HOLDER:
-                return before[:, :, CHUNK * c : CHUNK * (c + 1)]
-            if c == HOLDER:
-                return ends[:, 1:3, :]
-            if c < 6:
-                return after[:, :, CHUNK * (c - HOLDER - 1) : CHUNK * (c - HOLDER)]
-            return ends[:, c - 6 : 4 : 2, :]
+        def row2(c):
+            return c if c < EARLY else HOLDER - 1 + c - EARLY
 
+        def row3(c):
+            return EARLY + c % RING
 
-        def multiply(acc, m, first, n):
-            for c in range(n):
-                cols = slice(CHUNK * (first + c), CHUNK * (first + c + 1))
-                nc.tensor.matmul_mx(
-                    out=acc[:, CHUNK * c : CHUNK * (c + 1)],
-                    lhsT=w4[:, 256 * m : 256 * m + 256].bitcast(FP4X4),
-                    lhsT_scale=w4s[:, 128 * m : 128 * m + 128],
-                    rhs=codes[:, cols].bitcast(FP8X4),
-                    rhs_scale=scales[:, cols],
-                    start=c == 0,
-                    stop=False,
-                )
-            cols = slice(CHUNK * first, CHUNK * (first + n))
+        def gather3(c):
+            gather(late[:, row3(c), :], 3, CHUNK * c, CHUNK * (c + 1))
+
+        def multiply(acc, m, cols):
+            nc.tensor.matmul_mx(
+                out=acc,
+                lhsT=w4[:, 256 * m : 256 * m + 256].bitcast(FP4X4),
+                lhsT_scale=w4s[:, 128 * m : 128 * m + 128],
+                rhs=codes[:, cols].bitcast(FP8X4),
+                rhs_scale=scales[:, cols],
+                start=True,
+                stop=False,
+            )
             nc.tensor.matmul_mx(
                 out=acc,
                 lhsT=r8[:, 128 * m : 128 * m + 128].bitcast(FP8X4),
@@ -130,39 +124,43 @@ def tile_list_heads_none_kernel(
                 stop=True,
             )
 
-        groups = ((0, 1, (0, 1)), (1, 2, (2, 3)), (3, 1, (4,)), (4, 2, (5, 6)), (6, 1, (7, 0)), (7, 1, (1, 2)))
-        for first, n, names in groups:
-            w = n * CHUNK
-            split = len(names) == 2
-            if split:
-                banks = [psum.tile([P, w], F32, name=f"acc{b}")[:] for b in names]
+        banks = {}
+
+        def empty(c):
+            cols = slice(CHUNK * c, CHUNK * (c + 1))
+            res = keep.tile([P, 2, CHUNK], F32, name=f"res{c}", align_bytes=64)
+            if c == CHUNKS - 1:
+                for m, copy in enumerate((nc.scalar.copy, nc.vector.tensor_copy)):
+                    copy(res[:, m, :], banks[c][m])
+                    nc.sync.dma_start(out_halves[:, m, cols], res[:, m, :])
             else:
-                both = psum.tile([P, 2, w], F32, name=f"acc{names[0]}")
-                banks = [both[:, m, :] for m in range(2)]
-            res = keep.tile([P, 2, w], F32, name=f"res{first}", align_bytes=64)
-            for c in range(first, first + n):
-                cols = slice(CHUNK * c, CHUNK * (c + 1))
-                if c == 6:
-                    gather(ends[:, 0:2, :].rearrange("p r n -> p (r n)"), 2, 6 * CHUNK, S)
-                    gather(ends[:, 2:4, :].rearrange("p r n -> p (r n)"), 3, 6 * CHUNK, S)
-                elif c < 6:
-                    gather(pair(c)[:, 1, :], 3, cols.start, cols.stop)
-                copy = nc.vector.tensor_copy if c in ON_VECTOR else nc.scalar.copy
-                interleave(copy, pair(c), 1, cols.start, cols.stop)
-                nc.vector.quantize_mx(
-                    out=codes[:, cols].bitcast(FP8X4),
-                    scales=scales[:, cols],
-                    in_=xb[:, cols, :].rearrange("p n t -> p (n t)"),
-                )
+                (nc.vector.tensor_copy if c == CHUNKS - 2 else nc.scalar.copy)(res[:], banks[c][:])
+                nc.sync.dma_start(out_halves[:, :, cols], res[:])
+
+        for c in range(RING):
+            gather3(c)
+        for c in range(CHUNKS):
+            cols = slice(CHUNK * c, CHUNK * (c + 1))
+            copy = nc.vector.tensor_copy if c == CHUNKS - 1 else nc.scalar.copy
+            interleave(copy, late[:, row2(c) : row3(c) + 1 : row3(c) - row2(c), :], 1, cols.start, cols.stop)
+            if c >= LAG:
+                empty(c - LAG)
+            nc.vector.quantize_mx(
+                out=codes[:, cols].bitcast(FP8X4),
+                scales=scales[:, cols],
+                in_=xb[:, cols, :].rearrange("p n t -> p (n t)"),
+            )
+            if c + RING < CHUNKS:
+                gather3(c + RING)
+            if c == HOLDER:
+                gather(late[:, HOLDER - 1 : HOLDER + 1, :].rearrange("p r n -> p (r n)"), 2, EARLY * CHUNK, S)
+            if c == CHUNKS - 1:
+                halves = [psum.tile([P, CHUNK], F32, name=f"acc{b}")[:] for b in (c, 0)]
+                banks[c] = halves
+            else:
+                banks[c] = psum.tile([P, 2, CHUNK], F32, name=f"acc{c}")
+                halves = [banks[c][:, m, :] for m in range(2)]
             for m in range(2):
-                multiply(banks[m], m, first, n)
-            if split:
-                nc.scalar.copy(res[:, 0, :], banks[0])
-                (nc.vector.tensor_copy if first >= 6 else nc.scalar.copy)(res[:, 1, :], banks[1])
-            else:
-                nc.scalar.copy(res[:], both[:])
-            if split and first != 6:
-                for m in range(2):
-                    nc.sync.dma_start(out_halves[:, m, CHUNK * first : CHUNK * first + w], res[:, m, :])
-            else:
-                nc.sync.dma_start(out_halves[:, :, CHUNK * first : CHUNK * first + w], res[:])
+                multiply(halves[m], m, cols)
+        for c in range(CHUNKS - LAG, CHUNKS):
+            empty(c)

@@ -20,9 +20,12 @@ PACK = 4
 CHUNK = 128
 CHUNKS = S // CHUNK
 EARLY = 6
-RING = 3
-HOLDER = 2
-LAG = 3
+RING = 4
+HOLDER = 3
+LAG = 2
+ON_VECTOR = (1, 6, 7)
+GROUPS = ((0, 1, (0, 1)), (1, 2, (2, 3)), (3, 1, (4,)), (4, 2, (5, 6)), (6, 1, (7,)), (7, 1, (0, 1)))
+PIECES = ((0, 256), (256, 512), (512, 1024))
 
 
 def tile_list_heads_none_kernel(
@@ -62,12 +65,11 @@ def tile_list_heads_none_kernel(
         nc.sync.dma_start(rows[:], wgt.rearrange("p (h e) -> (p h) e", e=512)[0:256:17])
         nc.sync.dma_start(xs[0][:], planes[0])
         nc.sync.dma_start(offsets[:], offs)
-        for q in range(4):
-            load_scales(nc.gpsimd, w4s, w4_scales, q)
+        scale_loads = [(t, s, q) for t, s in ((r8s, r8_scales), (w4s, w4_scales)) for q in range(4)]
         for i in range(1, PACK):
             nc.sync.dma_start(xs[i][:], planes[i])
-            for q in ((0, 1), (2, 3), ())[i - 1]:
-                load_scales(nc.sync, r8s, r8_scales, q)
+            for tile, src, q in (scale_loads[:2], scale_loads[2:], ())[i - 1]:
+                load_scales(nc.sync, tile, src, q)
         nc.sync.dma_start(w4[:].bitcast(I32), w4_words[0].bitcast(I32))
         nc.sync.dma_start(r8[:].bitcast(I32), r8_words[0].rearrange("p n t -> p (n t)").bitcast(I32))
 
@@ -90,13 +92,13 @@ def tile_list_heads_none_kernel(
             copy(xb[:, a:b, 2 * h : 2 * h + 2], src.rearrange("p t n -> p n t"))
 
         gather(early[:, 0, :], 0, 0, S)
-        for a, b in ((0, 512), (512, 1024)):
+        for a, b in PIECES:
             gather(early[:, 1, a:b], 1, a, b)
             interleave(nc.scalar.copy, early[:, :, a:b], 0, a, b)
         gather(late[:, 0:EARLY, :].rearrange("p r n -> p (r n)"), 2, 0, EARLY * CHUNK)
 
         def row2(c):
-            return c if c < EARLY else HOLDER - 1 + c - EARLY
+            return c if c < EARLY else HOLDER + 1 + c - CHUNKS
 
         def row3(c):
             return EARLY + c % RING
@@ -104,16 +106,19 @@ def tile_list_heads_none_kernel(
         def gather3(c):
             gather(late[:, row3(c), :], 3, CHUNK * c, CHUNK * (c + 1))
 
-        def multiply(acc, m, cols):
-            nc.tensor.matmul_mx(
-                out=acc,
-                lhsT=w4[:, 256 * m : 256 * m + 256].bitcast(FP4X4),
-                lhsT_scale=w4s[:, 128 * m : 128 * m + 128],
-                rhs=codes[:, cols].bitcast(FP8X4),
-                rhs_scale=scales[:, cols],
-                start=True,
-                stop=False,
-            )
+        def multiply(acc, m, first, n):
+            for c in range(n):
+                cols = slice(CHUNK * (first + c), CHUNK * (first + c + 1))
+                nc.tensor.matmul_mx(
+                    out=acc[:, CHUNK * c : CHUNK * (c + 1)],
+                    lhsT=w4[:, 256 * m : 256 * m + 256].bitcast(FP4X4),
+                    lhsT_scale=w4s[:, 128 * m : 128 * m + 128],
+                    rhs=codes[:, cols].bitcast(FP8X4),
+                    rhs_scale=scales[:, cols],
+                    start=c == 0,
+                    stop=False,
+                )
+            cols = slice(CHUNK * first, CHUNK * (first + n))
             nc.tensor.matmul_mx(
                 out=acc,
                 lhsT=r8[:, 128 * m : 128 * m + 128].bitcast(FP8X4),
@@ -124,26 +129,29 @@ def tile_list_heads_none_kernel(
                 stop=True,
             )
 
-        banks = {}
+        ending = {first + n - 1: (first, n, names) for first, n, names in GROUPS}
+        filled = {}
 
         def empty(c):
-            cols = slice(CHUNK * c, CHUNK * (c + 1))
-            res = keep.tile([P, 2, CHUNK], F32, name=f"res{c}", align_bytes=64)
-            if c == CHUNKS - 1:
-                for m, copy in enumerate((nc.scalar.copy, nc.vector.tensor_copy)):
-                    copy(res[:, m, :], banks[c][m])
+            first, n, names = ending[c]
+            cols = slice(CHUNK * first, CHUNK * (c + 1))
+            res = keep.tile([P, 2, n * CHUNK], F32, name=f"res{c}", align_bytes=64)
+            if len(names) == 2:
+                for m in range(2):
+                    copy = nc.vector.tensor_copy if (c, m) in ((CHUNKS - 1, 1),) else nc.scalar.copy
+                    copy(res[:, m, :], filled[c][m])
                     nc.sync.dma_start(out_halves[:, m, cols], res[:, m, :])
             else:
-                (nc.vector.tensor_copy if c == CHUNKS - 2 else nc.scalar.copy)(res[:], banks[c][:])
+                (nc.vector.tensor_copy if c == CHUNKS - 2 else nc.scalar.copy)(res[:], filled[c][:])
                 nc.sync.dma_start(out_halves[:, :, cols], res[:])
 
         for c in range(RING):
             gather3(c)
         for c in range(CHUNKS):
             cols = slice(CHUNK * c, CHUNK * (c + 1))
-            copy = nc.vector.tensor_copy if c == CHUNKS - 1 else nc.scalar.copy
+            copy = nc.vector.tensor_copy if c in ON_VECTOR else nc.scalar.copy
             interleave(copy, late[:, row2(c) : row3(c) + 1 : row3(c) - row2(c), :], 1, cols.start, cols.stop)
-            if c >= LAG:
+            if c - LAG in ending:
                 empty(c - LAG)
             nc.vector.quantize_mx(
                 out=codes[:, cols].bitcast(FP8X4),
@@ -153,14 +161,17 @@ def tile_list_heads_none_kernel(
             if c + RING < CHUNKS:
                 gather3(c + RING)
             if c == HOLDER:
-                gather(late[:, HOLDER - 1 : HOLDER + 1, :].rearrange("p r n -> p (r n)"), 2, EARLY * CHUNK, S)
-            if c == CHUNKS - 1:
-                halves = [psum.tile([P, CHUNK], F32, name=f"acc{b}")[:] for b in (c, 0)]
-                banks[c] = halves
-            else:
-                banks[c] = psum.tile([P, 2, CHUNK], F32, name=f"acc{c}")
-                halves = [banks[c][:, m, :] for m in range(2)]
-            for m in range(2):
-                multiply(halves[m], m, cols)
+                gather(late[:, row2(EARLY) : row2(CHUNKS - 1) + 1, :].rearrange("p r n -> p (r n)"), 2, EARLY * CHUNK, S)
+            if c in ending:
+                first, n, names = ending[c]
+                if len(names) == 2:
+                    halves = [psum.tile([P, n * CHUNK], F32, name=f"acc{b}")[:] for b in names]
+                    filled[c] = halves
+                else:
+                    filled[c] = psum.tile([P, 2, n * CHUNK], F32, name=f"acc{names[0]}")
+                    halves = [filled[c][:, m, :] for m in range(2)]
+                for m in range(2):
+                    multiply(halves[m], m, first, n)
         for c in range(CHUNKS - LAG, CHUNKS):
-            empty(c)
+            if c in ending:
+                empty(c)

@@ -65,13 +65,14 @@ def tile_list_heads_none_kernel(
         nc.sync.dma_start(rows[:], wgt.rearrange("p (h e) -> (p h) e", e=512)[0:256:17])
         nc.sync.dma_start(xs[0][:], planes[0])
         nc.sync.dma_start(offsets[:], offs)
-        scale_loads = [(t, s, q) for t, s in ((r8s, r8_scales), (w4s, w4_scales)) for q in range(4)]
         for i in range(1, PACK):
             nc.sync.dma_start(xs[i][:], planes[i])
-            for tile, src, q in (scale_loads[:2], scale_loads[2:], ())[i - 1]:
-                load_scales(nc.sync, tile, src, q)
+            for q in ((0, 1), (2,), (3,))[i - 1]:
+                load_scales(nc.sync, r8s, r8_scales, q)
         nc.sync.dma_start(w4[:].bitcast(I32), w4_words[0].bitcast(I32))
         nc.sync.dma_start(r8[:].bitcast(I32), r8_words[0].rearrange("p n t -> p (n t)").bitcast(I32))
+        for q in range(4):
+            load_scales(nc.sync, w4s, w4_scales, q)
 
         for a in (0, 32):
             nc.vector.transpose(turned[:, a : a + 32], rows[:, a : a + 32])

@@ -20,12 +20,12 @@ PACK = 4
 CHUNK = 128
 CHUNKS = S // CHUNK
 EARLY = 6
-RING = 4
+GATHERS = ((0, 1, 9, None), (1, 1, 6, None), (2, 2, 7, None), (4, 2, 9, 0), (6, 2, 6, 2))
 HOLDER = 3
-LAG = 2
-ON_VECTOR = (1, 6, 7)
+LAG = 1
+ON_VECTOR = (6, 7)
 GROUPS = ((0, 1, (0, 1)), (1, 2, (2, 3)), (3, 1, (4,)), (4, 2, (5, 6)), (6, 1, (7,)), (7, 1, (0, 1)))
-PIECES = ((0, 256), (256, 512), (512, 1024))
+PIECES = ((0, 384), (384, 1024))
 
 
 def tile_list_heads_none_kernel(
@@ -48,7 +48,7 @@ def tile_list_heads_none_kernel(
         w4s = keep.tile([P, M], U8, name="w4s", align_bytes=64)
         r8s = keep.tile([P, M], U8, name="r8s", align_bytes=64)
         early = keep.tile([P, 2, S], F32, name="early", align_bytes=64)
-        late = keep.tile([P, EARLY + RING, CHUNK], F32, name="late", align_bytes=64)
+        late = keep.tile([P, 11, CHUNK], F32, name="late", align_bytes=64)
         xb = keep.tile([P, S, PACK], BF16, name="xb", align_bytes=64)
         codes = keep.tile([P, S], U32, name="codes", align_bytes=64)
         scales = keep.tile([P, S], U8, name="scales", align_bytes=64)
@@ -102,10 +102,10 @@ def tile_list_heads_none_kernel(
             return c if c < EARLY else HOLDER + 1 + c - CHUNKS
 
         def row3(c):
-            return EARLY + c % RING
+            return [row + c - first for first, n, row, after in GATHERS if first <= c < first + n][0]
 
-        def gather3(c):
-            gather(late[:, row3(c), :], 3, CHUNK * c, CHUNK * (c + 1))
+        def gather3(first, n, row):
+            gather(late[:, row : row + n, :].rearrange("p r n -> p (r n)"), 3, CHUNK * first, CHUNK * (first + n))
 
         def multiply(acc, m, first, n):
             for c in range(n):
@@ -146,10 +146,11 @@ def tile_list_heads_none_kernel(
                 (nc.vector.tensor_copy if c == CHUNKS - 2 else nc.scalar.copy)(res[:], filled[c][:])
                 nc.sync.dma_start(out_halves[:, :, cols], res[:])
 
-        for c in range(RING):
-            gather3(c)
         for c in range(CHUNKS):
             cols = slice(CHUNK * c, CHUNK * (c + 1))
+            for first, n, row, after in GATHERS:
+                if first == c and after is None:
+                    gather3(first, n, row)
             copy = nc.vector.tensor_copy if c in ON_VECTOR else nc.scalar.copy
             interleave(copy, late[:, row2(c) : row3(c) + 1 : row3(c) - row2(c), :], 1, cols.start, cols.stop)
             if c - LAG in ending:
@@ -159,8 +160,9 @@ def tile_list_heads_none_kernel(
                 scales=scales[:, cols],
                 in_=xb[:, cols, :].rearrange("p n t -> p (n t)"),
             )
-            if c + RING < CHUNKS:
-                gather3(c + RING)
+            for first, n, row, after in GATHERS:
+                if after == c:
+                    gather3(first, n, row)
             if c == HOLDER:
                 gather(late[:, row2(EARLY) : row2(CHUNKS - 1) + 1, :].rearrange("p r n -> p (r n)"), 2, EARLY * CHUNK, S)
             if c in ending:

@@ -24,7 +24,7 @@ GATHERS = ((0, 1, 9, None), (1, 1, 6, None), (2, 2, 7, None), (4, 2, 9, 0), (6, 
 HOLDER = 3
 LAG = 1
 ON_VECTOR = (6, 7)
-GROUPS = ((0, 1, (0, 1)), (1, 2, (2, 3)), (3, 1, (4,)), (4, 2, (5, 6)), (6, 1, (7,)), (7, 1, (0, 1)))
+GROUPS = ((0, 1, (0, 1)), (1, 2, (2, 3)), (3, 1, (4,)), (4, 2, (5, 6)), (6, 1, (7, 0)), (7, 1, (1, 2)))
 PIECES = ((0, 384), (384, 1024))
 
 
@@ -139,11 +139,12 @@ def tile_list_heads_none_kernel(
             res = keep.tile([P, 2, n * CHUNK], F32, name=f"res{c}", align_bytes=64)
             if len(names) == 2:
                 for m in range(2):
-                    copy = nc.vector.tensor_copy if (c, m) in ((CHUNKS - 1, 1),) else nc.scalar.copy
+                    copy = nc.vector.tensor_copy if (c, m) in ((5, 1), (6, 1), (7, 1)) else nc.scalar.copy
                     copy(res[:, m, :], filled[c][m])
-                    nc.sync.dma_start(out_halves[:, m, cols], res[:, m, :])
+                    queue = nc.scalar if (c, m) == (CHUNKS - 1, 0) else nc.sync
+                    queue.dma_start(out_halves[:, m, cols], res[:, m, :])
             else:
-                (nc.vector.tensor_copy if c == CHUNKS - 2 else nc.scalar.copy)(res[:], filled[c][:])
+                nc.scalar.copy(res[:], filled[c][:])
                 nc.sync.dma_start(out_halves[:, :, cols], res[:])
 
         for c in range(CHUNKS):

@@ -24,7 +24,7 @@ GATHERS = ((0, 1, 9, None), (1, 1, 6, None), (2, 2, 7, None), (4, 2, 9, 0), (6, 
 HOLDER = 3
 LAG = 1
 ON_VECTOR = (6, 7)
-GROUPS = ((0, 1, (0, 1)), (1, 2, (2, 3)), (3, 1, (4,)), (4, 2, (5, 6)), (6, 1, (7, 0)), (7, 1, (1, 2)))
+GROUPS = ((0, 1, (0,)), (1, 2, (1, 2)), (3, 1, (3,)), (4, 2, (4, 5)), (6, 1, (6, 7)), (7, 1, (0, 1)))
 PIECES = ((0, 384), (384, 1024))
 
 
@@ -141,8 +141,10 @@ def tile_list_heads_none_kernel(
                 for m in range(2):
                     copy = nc.vector.tensor_copy if (c, m) in ((5, 1), (6, 1), (7, 1)) else nc.scalar.copy
                     copy(res[:, m, :], filled[c][m])
-                    queue = nc.scalar if (c, m) == (CHUNKS - 1, 0) else nc.sync
-                    queue.dma_start(out_halves[:, m, cols], res[:, m, :])
+                    if c in (5, 7):
+                        nc.sync.dma_start(out_halves[:, m, cols], res[:, m, :])
+                if c not in (5, 7):
+                    nc.sync.dma_start(out_halves[:, :, cols], res[:])
             else:
                 nc.scalar.copy(res[:], filled[c][:])
                 nc.sync.dma_start(out_halves[:, :, cols], res[:])

@@ -92,10 +92,16 @@ def tile_list_heads_none_kernel(
         def interleave(copy, src, h, a, b):
             copy(xb[:, a:b, 2 * h : 2 * h + 2], src.rearrange("p t n -> p n t"))
 
+        def interleave_by_fours(copy, src, h, a, b):
+            copy(
+                xb[:, a:b, 2 * h : 2 * h + 2].rearrange("p (c i) t -> p c t i", i=4),
+                src.rearrange("p t (c i) -> p c t i", i=4),
+            )
+
         gather(early[:, 0, :], 0, 0, S)
         for a, b in PIECES:
             gather(early[:, 1, a:b], 1, a, b)
-            interleave(nc.scalar.copy, early[:, :, a:b], 0, a, b)
+            interleave_by_fours(nc.scalar.copy, early[:, :, a:b], 0, a, b)
         gather(late[:, 0:EARLY, :].rearrange("p r n -> p (r n)"), 2, 0, EARLY * CHUNK)
 
         def row2(c):
@@ -155,7 +161,7 @@ def tile_list_heads_none_kernel(
                 if first == c and after is None:
                     gather3(first, n, row)
             copy = nc.vector.tensor_copy if c in ON_VECTOR else nc.scalar.copy
-            interleave(copy, late[:, row2(c) : row3(c) + 1 : row3(c) - row2(c), :], 1, cols.start, cols.stop)
+            (interleave_by_fours if c in ON_VECTOR else interleave)(copy, late[:, row2(c) : row3(c) + 1 : row3(c) - row2(c), :], 1, cols.start, cols.stop)
             if c - LAG in ending:
                 empty(c - LAG)
             nc.vector.quantize_mx(

@@ -19,12 +19,6 @@ P = 128
 PACK = 4
 CHUNK = 128
 CHUNKS = S // CHUNK
-EARLY = 6
-GATHERS = ((0, 1, 9, None), (1, 1, 6, None), (2, 2, 7, None), (4, 2, 9, 0), (6, 2, 6, 2))
-HOLDER = 3
-LAG = 1
-ON_VECTOR = (6, 7)
-GROUPS = ((0, 1, (0,)), (1, 2, (1, 2)), (3, 1, (3,)), (4, 2, (4, 5)), (6, 1, (6, 7)), (7, 1, (0, 1)))
 PIECES = ((0, 384), (384, 1024))
 
 
@@ -65,10 +59,12 @@ def tile_list_heads_none_kernel(
         nc.sync.dma_start(rows[:], wgt.rearrange("p (h e) -> (p h) e", e=512)[0:256:17])
         nc.sync.dma_start(xs[0][:], planes[0])
         nc.sync.dma_start(offsets[:], offs)
+        for q in range(1):
+            load_scales(nc.gpsimd, r8s, r8_scales, q)
         for i in range(1, PACK):
             nc.sync.dma_start(xs[i][:], planes[i])
-            for q in ((0, 1), (2,), (3,))[i - 1]:
-                load_scales(nc.sync, r8s, r8_scales, q)
+            if i >= 1:
+                load_scales(nc.sync, r8s, r8_scales, i)
         nc.sync.dma_start(w4[:].bitcast(I32), w4_words[0].bitcast(I32))
         nc.sync.dma_start(r8[:].bitcast(I32), r8_words[0].rearrange("p n t -> p (n t)").bitcast(I32))
         for q in range(4):
@@ -102,17 +98,6 @@ def tile_list_heads_none_kernel(
         for a, b in PIECES:
             gather(early[:, 1, a:b], 1, a, b)
             interleave_by_fours(nc.scalar.copy, early[:, :, a:b], 0, a, b)
-        gather(late[:, 0:EARLY, :].rearrange("p r n -> p (r n)"), 2, 0, EARLY * CHUNK)
-
-        def row2(c):
-            return c if c < EARLY else HOLDER + 1 + c - CHUNKS
-
-        def row3(c):
-            return [row + c - first for first, n, row, after in GATHERS if first <= c < first + n][0]
-
-        def gather3(first, n, row):
-            gather(late[:, row : row + n, :].rearrange("p r n -> p (r n)"), 3, CHUNK * first, CHUNK * (first + n))
-
         def multiply(acc, m, first, n):
             for c in range(n):
                 cols = slice(CHUNK * (first + c), CHUNK * (first + c + 1))
@@ -136,54 +121,84 @@ def tile_list_heads_none_kernel(
                 stop=True,
             )
 
-        ending = {first + n - 1: (first, n, names) for first, n, names in GROUPS}
-        filled = {}
+        row = {}
 
-        def empty(c):
-            first, n, names = ending[c]
-            cols = slice(CHUNK * first, CHUNK * (c + 1))
-            res = keep.tile([P, 2, n * CHUNK], F32, name=f"res{c}", align_bytes=64)
-            if len(names) == 2:
-                for m in range(2):
-                    copy = nc.vector.tensor_copy if (c, m) in ((5, 1), (6, 1), (7, 1)) else nc.scalar.copy
-                    copy(res[:, m, :], filled[c][m])
-                    if c in (5, 7):
-                        nc.sync.dma_start(out_halves[:, m, cols], res[:, m, :])
-                if c not in (5, 7):
-                    nc.sync.dma_start(out_halves[:, :, cols], res[:])
-            else:
-                nc.scalar.copy(res[:], filled[c][:])
-                nc.sync.dma_start(out_halves[:, :, cols], res[:])
+        def late_gather(plane, first, n, at):
+            for c in range(n):
+                row[plane, first + c] = at + c
+            gather(late[:, at : at + n, :].rearrange("p r n -> p (r n)"), plane, CHUNK * first, CHUNK * (first + n))
 
-        for c in range(CHUNKS):
+        def weave(copy, c):
+            lo, hi = row[2, c], row[3, c]
+            interleave(copy, late[:, lo : hi + 1 : hi - lo, :], 1, CHUNK * c, CHUNK * (c + 1))
+
+        def quantize(c):
             cols = slice(CHUNK * c, CHUNK * (c + 1))
-            for first, n, row, after in GATHERS:
-                if first == c and after is None:
-                    gather3(first, n, row)
-            copy = nc.vector.tensor_copy if c in ON_VECTOR else nc.scalar.copy
-            (interleave_by_fours if c in ON_VECTOR else interleave)(copy, late[:, row2(c) : row3(c) + 1 : row3(c) - row2(c), :], 1, cols.start, cols.stop)
-            if c - LAG in ending:
-                empty(c - LAG)
             nc.vector.quantize_mx(
                 out=codes[:, cols].bitcast(FP8X4),
                 scales=scales[:, cols],
                 in_=xb[:, cols, :].rearrange("p n t -> p (n t)"),
             )
-            for first, n, row, after in GATHERS:
-                if after == c:
-                    gather3(first, n, row)
-            if c == HOLDER:
-                gather(late[:, row2(EARLY) : row2(CHUNKS - 1) + 1, :].rearrange("p r n -> p (r n)"), 2, EARLY * CHUNK, S)
-            if c in ending:
-                first, n, names = ending[c]
-                if len(names) == 2:
-                    halves = [psum.tile([P, n * CHUNK], F32, name=f"acc{b}")[:] for b in names]
-                    filled[c] = halves
-                else:
-                    filled[c] = psum.tile([P, 2, n * CHUNK], F32, name=f"acc{names[0]}")
-                    halves = [filled[c][:, m, :] for m in range(2)]
+
+        def product(first, n, banks):
+            if len(banks) == 2:
+                halves = [psum.tile([P, n * CHUNK], F32, name=f"acc{b}")[:] for b in banks]
+                whole = None
+            else:
+                whole = psum.tile([P, 2, n * CHUNK], F32, name=f"acc{banks[0]}")
+                halves = [whole[:, m, :] for m in range(2)]
+            for m in range(2):
+                multiply(halves[m], m, first, n)
+            return first, n, halves, whole
+
+        def empty(group, copies, split):
+            first, n, halves, whole = group
+            cols = slice(CHUNK * first, CHUNK * (first + n))
+            res = keep.tile([P, 2, n * CHUNK], F32, name=f"res{first}", align_bytes=64)
+            if whole is not None:
+                copies[0](res[:], whole[:])
+            else:
                 for m in range(2):
-                    multiply(halves[m], m, first, n)
-        for c in range(CHUNKS - LAG, CHUNKS):
-            if c in ending:
-                empty(c)
+                    copies[m](res[:, m, :], halves[m])
+                    if split:
+                        nc.sync.dma_start(out_halves[:, m, cols], res[:, m, :])
+            if not split:
+                nc.sync.dma_start(out_halves[:, :, cols], res[:])
+
+        act, dve = nc.scalar.copy, nc.vector.tensor_copy
+
+        late_gather(2, 0, 6, 0)
+        late_gather(3, 0, 1, 9)
+        late_gather(3, 1, 1, 6)
+        late_gather(3, 2, 2, 7)
+        weave(act, 0)
+        quantize(0)
+        late_gather(3, 4, 2, 9)
+        g0 = product(0, 1, (0,))
+        weave(act, 1)
+        empty(g0, (act,), False)
+        quantize(1)
+        weave(act, 2)
+        quantize(2)
+        late_gather(3, 6, 2, 6)
+        g1 = product(1, 2, (1, 2))
+        weave(act, 3)
+        empty(g1, (act, act), True)
+        quantize(3)
+        late_gather(2, 6, 2, 2)
+        g3 = product(3, 1, (3,))
+        weave(act, 4)
+        empty(g3, (act,), False)
+        quantize(4)
+        weave(act, 5)
+        quantize(5)
+        g4 = product(4, 2, (4, 5))
+        weave(dve, 6)
+        empty(g4, (act, dve), True)
+        quantize(6)
+        g6 = product(6, 1, (6, 7))
+        weave(dve, 7)
+        empty(g6, (act, dve), False)
+        quantize(7)
+        g7 = product(7, 1, (0, 1))
+        empty(g7, (act, dve), True)

@@ -59,12 +59,10 @@ def tile_list_heads_none_kernel(
         nc.sync.dma_start(rows[:], wgt.rearrange("p (h e) -> (p h) e", e=512)[0:256:17])
         nc.sync.dma_start(xs[0][:], planes[0])
         nc.sync.dma_start(offsets[:], offs)
-        for q in range(1):
-            load_scales(nc.gpsimd, r8s, r8_scales, q)
         for i in range(1, PACK):
             nc.sync.dma_start(xs[i][:], planes[i])
-            if i >= 1:
-                load_scales(nc.sync, r8s, r8_scales, i)
+            for q in ((0, 1), (2,), (3,))[i - 1]:
+                load_scales(nc.sync, r8s, r8_scales, q)
         nc.sync.dma_start(w4[:].bitcast(I32), w4_words[0].bitcast(I32))
         nc.sync.dma_start(r8[:].bitcast(I32), r8_words[0].rearrange("p n t -> p (n t)").bitcast(I32))
         for q in range(4):
@@ -201,4 +199,4 @@ def tile_list_heads_none_kernel(
         empty(g6, (act, dve), False)
         quantize(7)
         g7 = product(7, 1, (0, 1))
-        empty(g7, (act, dve), True)
+        empty(g7, (act, dve), False)

@@ -165,6 +165,13 @@ def tile_list_heads_none_kernel(
 
         act, dve = nc.scalar.copy, nc.vector.tensor_copy
 
+        def product_by_chunks(halves, first, c):
+            for m in range(2):
+                multiply(halves[m][:, CHUNK * c : CHUNK * (c + 1)], m, first + c, 1)
+
+        def banks_of(banks, n):
+            return [psum.tile([P, n * CHUNK], F32, name=f"acc{b}")[:] for b in banks]
+
         late_gather(2, 0, 6, 0)
         late_gather(3, 0, 1, 9)
         late_gather(3, 1, 1, 6)
@@ -172,21 +179,23 @@ def tile_list_heads_none_kernel(
         weave(act, 0)
         quantize(0)
         late_gather(3, 4, 2, 9)
-        g0 = product(0, 1, (0,))
+        h0 = banks_of((0, 1), 2)
+        product_by_chunks(h0, 0, 0)
         weave(act, 1)
-        empty(g0, (act,), False)
         quantize(1)
+        product_by_chunks(h0, 0, 1)
         weave(act, 2)
+        empty((0, 2, h0, None), (act, act), True)
         quantize(2)
         late_gather(3, 6, 2, 6)
-        g1 = product(1, 2, (1, 2))
+        h2 = banks_of((2, 3), 2)
+        product_by_chunks(h2, 2, 0)
         weave(act, 3)
-        empty(g1, (act, act), True)
         quantize(3)
         late_gather(2, 6, 2, 2)
-        g3 = product(3, 1, (3,))
+        product_by_chunks(h2, 2, 1)
         weave(act, 4)
-        empty(g3, (act,), False)
+        empty((2, 2, h2, None), (act, act), True)
         quantize(4)
         weave(act, 5)
         quantize(5)

@@ -201,11 +201,13 @@ def tile_list_heads_none_kernel(
         quantize(5)
         g4 = product(4, 2, (4, 5))
         weave(dve, 6)
-        empty(g4, (act, dve), True)
+        empty(g4, (act, act), True)
         quantize(6)
-        g6 = product(6, 1, (6, 7))
         weave(dve, 7)
-        empty(g6, (act, dve), False)
         quantize(7)
-        g7 = product(7, 1, (0, 1))
-        empty(g7, (act, dve), False)
+        res6 = keep.tile([P, 2, 2 * CHUNK], F32, name="res6", align_bytes=64)
+        for m, (copy, banks) in enumerate(((dve, (6, 7)), (act, (0, 1)))):
+            for c, acc in enumerate(banks_of(banks, 1)):
+                multiply(acc, m, 6 + c, 1)
+                copy(res6[:, m, CHUNK * c : CHUNK * (c + 1)], acc)
+            nc.sync.dma_start(out_halves[:, m, 6 * CHUNK :], res6[:, m, :])

@@ -35,17 +35,17 @@ def tile_list_heads_none_kernel(
         psum = ctx.enter_context(tc.psum_pool(name="psum", bufs=1))
 
         offsets = lists.tile([P, S // 16], U16, name="offsets")
-        weight = keep.tile([P, S], F32, name="weight", align_bytes=64)
-        xs = [keep.tile([P, T], F32, name=f"x{i}", align_bytes=64) for i in range(PACK)]
-        w4 = keep.tile([P, 2 * M], U8, name="w4", align_bytes=64)
-        r8 = keep.tile([P, M], U32, name="r8", align_bytes=64)
-        w4s = keep.tile([P, M], U8, name="w4s", align_bytes=64)
-        r8s = keep.tile([P, M], U8, name="r8s", align_bytes=64)
-        early = keep.tile([P, 2, S], F32, name="early", align_bytes=64)
-        late = keep.tile([P, 11, CHUNK], F32, name="late", align_bytes=64)
-        xb = keep.tile([P, S, PACK], BF16, name="xb", align_bytes=64)
-        codes = keep.tile([P, S], U32, name="codes", align_bytes=64)
-        scales = keep.tile([P, S], U8, name="scales", align_bytes=64)
+        weight = keep.tile([P, S], F32, name="weight", align_bytes=64, offset=131072)
+        xs = [keep.tile([P, T], F32, name=f"x{i}", align_bytes=64, offset=65536 * (i % 2) + 8192 * (i // 2)) for i in range(PACK)]
+        w4 = keep.tile([P, 2 * M], U8, name="w4", align_bytes=64, offset=229376)
+        r8 = keep.tile([P, M], U32, name="r8", align_bytes=64, offset=230400)
+        w4s = keep.tile([P, M], U8, name="w4s", align_bytes=64, offset=231424)
+        r8s = keep.tile([P, M], U8, name="r8s", align_bytes=64, offset=231680)
+        early = keep.tile([P, 2, S], F32, name="early", align_bytes=64, offset=196608)
+        late = keep.tile([P, 11, CHUNK], F32, name="late", align_bytes=64, offset=204800)
+        xb = keep.tile([P, S, PACK], BF16, name="xb", align_bytes=64, offset=163840)
+        codes = keep.tile([P, S], U32, name="codes", align_bytes=64, offset=233472)
+        scales = keep.tile([P, S], U8, name="scales", align_bytes=64, offset=237568)
 
         nc.vector.memset(r8s[:].bitcast(I32), 0)
         nc.vector.memset(w4s[:].bitcast(I32), 0)
@@ -53,9 +53,9 @@ def tile_list_heads_none_kernel(
         def load_scales(engine, tile, src, q):
             engine.dma_start(tile[32 * q : 32 * q + 4, :].bitcast(I32), src[0, 4 * q : 4 * q + 4, :].bitcast(I32))
 
-        rows = keep.tile([P, 64], F32, name="rows", align_bytes=64)
-        turned = keep.tile([P, 64], F32, name="turned", align_bytes=64)
-        spread = keep.tile([P, S], F32, name="spread", align_bytes=64)
+        rows = keep.tile([P, 64], F32, name="rows", align_bytes=64, offset=40960)
+        turned = keep.tile([P, 64], F32, name="turned", align_bytes=64, offset=41984)
+        spread = keep.tile([P, S], F32, name="spread", align_bytes=64, offset=43008)
         nc.sync.dma_start(rows[:], wgt.rearrange("p (h e) -> (p h) e", e=512)[0:256:17])
         nc.sync.dma_start(xs[0][:], planes[0])
         nc.sync.dma_start(offsets[:], offs)
@@ -152,7 +152,7 @@ def tile_list_heads_none_kernel(
         def empty(group, copies, split):
             first, n, halves, whole = group
             cols = slice(CHUNK * first, CHUNK * (first + n))
-            res = keep.tile([P, 2, n * CHUNK], F32, name=f"res{first}", align_bytes=64)
+            res = keep.tile([P, 2, n * CHUNK], F32, name=f"res{first}", align_bytes=64, offset=16384 + 1024 * first)
             if whole is not None:
                 copies[0](res[:], whole[:])
             else:
@@ -205,7 +205,7 @@ def tile_list_heads_none_kernel(
         quantize(6)
         weave(dve, 7)
         quantize(7)
-        res6 = keep.tile([P, 2, 2 * CHUNK], F32, name="res6", align_bytes=64)
+        res6 = keep.tile([P, 2, 2 * CHUNK], F32, name="res6", align_bytes=64, offset=22528)
         for m, (copy, banks) in enumerate(((dve, (6, 7)), (act, (0, 1)))):
             for c, acc in enumerate(banks_of(banks, 1)):
                 multiply(acc, m, 6 + c, 1)

@@ -37,15 +37,15 @@ def tile_list_heads_none_kernel(
         offsets = lists.tile([P, S // 16], U16, name="offsets")
         weight = keep.tile([P, S], F32, name="weight", align_bytes=64, offset=131072)
         xs = [keep.tile([P, T], F32, name=f"x{i}", align_bytes=64, offset=65536 * (i % 2) + 8192 * (i // 2)) for i in range(PACK)]
-        w4 = keep.tile([P, 2 * M], U8, name="w4", align_bytes=64, offset=229376)
-        r8 = keep.tile([P, M], U32, name="r8", align_bytes=64, offset=230400)
-        w4s = keep.tile([P, M], U8, name="w4s", align_bytes=64, offset=231424)
-        r8s = keep.tile([P, M], U8, name="r8s", align_bytes=64, offset=231680)
-        early = keep.tile([P, 2, S], F32, name="early", align_bytes=64, offset=196608)
-        late = keep.tile([P, 11, CHUNK], F32, name="late", align_bytes=64, offset=204800)
+        w4 = keep.tile([P, 2 * M], U8, name="w4", align_bytes=64, offset=106496)
+        r8 = keep.tile([P, M], U32, name="r8", align_bytes=64, offset=107520)
+        w4s = keep.tile([P, M], U8, name="w4s", align_bytes=64, offset=108544)
+        r8s = keep.tile([P, M], U8, name="r8s", align_bytes=64, offset=108800)
+        early = keep.tile([P, 2, S], F32, name="early", align_bytes=64, offset=98304)
+        late = keep.tile([P, 11, CHUNK], F32, name="late", align_bytes=64, offset=196608)
         xb = keep.tile([P, S, PACK], BF16, name="xb", align_bytes=64, offset=163840)
-        codes = keep.tile([P, S], U32, name="codes", align_bytes=64, offset=233472)
-        scales = keep.tile([P, S], U8, name="scales", align_bytes=64, offset=237568)
+        codes = keep.tile([P, S], U32, name="codes", align_bytes=64, offset=229376)
+        scales = keep.tile([P, S], U8, name="scales", align_bytes=64, offset=139264)
 
         nc.vector.memset(r8s[:].bitcast(I32), 0)
         nc.vector.memset(w4s[:].bitcast(I32), 0)
@@ -152,7 +152,7 @@ def tile_list_heads_none_kernel(
         def empty(group, copies, split):
             first, n, halves, whole = group
             cols = slice(CHUNK * first, CHUNK * (first + n))
-            res = keep.tile([P, 2, n * CHUNK], F32, name=f"res{first}", align_bytes=64, offset=16384 + 1024 * first)
+            res = keep.tile([P, 2, n * CHUNK], F32, name=f"res{first}", align_bytes=64, offset=32768 + 1024 * first)
             if whole is not None:
                 copies[0](res[:], whole[:])
             else:
@@ -205,7 +205,7 @@ def tile_list_heads_none_kernel(
         quantize(6)
         weave(dve, 7)
         quantize(7)
-        res6 = keep.tile([P, 2, 2 * CHUNK], F32, name="res6", align_bytes=64, offset=22528)
+        res6 = keep.tile([P, 2, 2 * CHUNK], F32, name="res6", align_bytes=64, offset=38912)
         for m, (copy, banks) in enumerate(((dve, (6, 7)), (act, (0, 1)))):
             for c, acc in enumerate(banks_of(banks, 1)):
                 multiply(acc, m, 6 + c, 1)

@@ -17,92 +17,144 @@ MULT = mybir.AluOpType.mult
 
 P = 128
 PACK = 4
+HALVES = M // P
 CHUNK = 128
 CHUNKS = S // CHUNK
-PIECES = ((0, 384), (384, 1024))
+PAIR = 2 * CHUNK
+
+FIRST_PIECE = 384
+EARLY_CHUNKS = 6
+SCALAR_CHUNKS = 6
+FIRST_GATHERS = (1, 1, 2)
+HELD_GATHERS = {0: (3, 4), 2: (3, 6), 3: (2, 6)}
+HALF_BY_HALF_PAIR = 2
+
+KIB = 1024
+ZONE = 32 * KIB
+RESERVED = 16 * KIB
+WEIGHT_ZONE, EARLY_ZONE, LATE_ZONE, WOVEN_ZONE, CODES_ZONE, SPARE_ZONE = 0, 3, 4, 5, 6, 7
+PLANE_ZONES = (1, 2)
+RESULT_ZONES = (SPARE_ZONE, EARLY_ZONE, PLANE_ZONES[1], PLANE_ZONES[0])
 
 
 def tile_list_heads_none_kernel(
     tc, xT, w4_words, w4_scales, r8_words, r8_scales, wgt, offs, out
 ):
     nc = tc.nc
-    planes = xT.rearrange("(p i) t -> i p t", i=PACK)
+    plane_rows = xT.rearrange("(p i) t -> i p t", i=PACK)
     out_halves = out.rearrange("(m p) j -> p m j", p=P)
+    on_scalar, on_vector = nc.scalar.copy, nc.vector.tensor_copy
 
     with ExitStack() as ctx:
         lists = ctx.enter_context(tc.tile_pool(name="lists", bufs=1))
         keep = ctx.enter_context(tc.tile_pool(name="keep", bufs=1))
         psum = ctx.enter_context(tc.psum_pool(name="psum", bufs=1))
 
+        filled = {}
+
+        def place(name, shape, dtype, itemsize, zone):
+            used = filled.get(zone, 0)
+            size = itemsize
+            for n in shape[1:]:
+                size = size * n
+            filled[zone] = used + size
+            start = max(zone * ZONE - RESERVED, 0)
+            return keep.tile(shape, dtype, name=name, align_bytes=64, offset=start + used)
+
         offsets = lists.tile([P, S // 16], U16, name="offsets")
-        weight = keep.tile([P, S], F32, name="weight", align_bytes=64, offset=131072)
-        xs = [keep.tile([P, T], F32, name=f"x{i}", align_bytes=64, offset=65536 * (i % 2) + 8192 * (i // 2)) for i in range(PACK)]
-        w4 = keep.tile([P, 2 * M], U8, name="w4", align_bytes=64, offset=106496)
-        r8 = keep.tile([P, M], U32, name="r8", align_bytes=64, offset=107520)
-        w4s = keep.tile([P, M], U8, name="w4s", align_bytes=64, offset=108544)
-        r8s = keep.tile([P, M], U8, name="r8s", align_bytes=64, offset=108800)
-        early = keep.tile([P, 2, S], F32, name="early", align_bytes=64, offset=98304)
-        late = keep.tile([P, 11, CHUNK], F32, name="late", align_bytes=64, offset=196608)
-        xb = keep.tile([P, S, PACK], BF16, name="xb", align_bytes=64, offset=163840)
-        codes = keep.tile([P, S], U32, name="codes", align_bytes=64, offset=229376)
-        scales = keep.tile([P, S], U8, name="scales", align_bytes=64, offset=139264)
+        weight = place("weight", [P, S], F32, 4, WEIGHT_ZONE)
+        rows = place("rows", [P, 64], F32, 4, WEIGHT_ZONE)
+        turned = place("turned", [P, 64], F32, 4, WEIGHT_ZONE)
+        spread = place("spread", [P, S], F32, 4, WEIGHT_ZONE)
+        planes = [place(f"plane{i}", [P, T], F32, 4, PLANE_ZONES[i % 2]) for i in range(PACK)]
+        early = place("early", [P, 2, S], F32, 4, EARLY_ZONE)
+        w4 = place("w4", [P, 2 * M], U8, 1, EARLY_ZONE)
+        r8 = place("r8", [P, M], U32, 4, EARLY_ZONE)
+        w4s = place("w4s", [P, M], U8, 1, EARLY_ZONE)
+        r8s = place("r8s", [P, M], U8, 1, EARLY_ZONE)
+        strips = EARLY_CHUNKS + sum(FIRST_GATHERS) + 1
+        late = place("late", [P, strips, CHUNK], F32, 4, LATE_ZONE)
+        pieces = ((0, FIRST_PIECE, SPARE_ZONE), (FIRST_PIECE, S, WOVEN_ZONE))
+        xb_parts = [place(f"xb{a}", [P, b - a, PACK], BF16, 2, zone) for a, b, zone in pieces]
+        codes = place("codes", [P, S], U32, 4, CODES_ZONE)
+        scales = place("scales", [P, S], U8, 1, CODES_ZONE)
+        results = [
+            place(f"result{n}", [P, PAIR], F32, 4, RESULT_ZONES[n % len(RESULT_ZONES)])
+            for n in range(HALVES * CHUNKS // 2)
+        ]
 
         nc.vector.memset(r8s[:].bitcast(I32), 0)
         nc.vector.memset(w4s[:].bitcast(I32), 0)
 
-        def load_scales(engine, tile, src, q):
-            engine.dma_start(tile[32 * q : 32 * q + 4, :].bitcast(I32), src[0, 4 * q : 4 * q + 4, :].bitcast(I32))
+        def load_scales(tile, src, q):
+            nc.sync.dma_start(tile[32 * q : 32 * q + 4, :].bitcast(I32), src[0, 4 * q : 4 * q + 4, :].bitcast(I32))
 
-        rows = keep.tile([P, 64], F32, name="rows", align_bytes=64, offset=40960)
-        turned = keep.tile([P, 64], F32, name="turned", align_bytes=64, offset=41984)
-        spread = keep.tile([P, S], F32, name="spread", align_bytes=64, offset=43008)
         nc.sync.dma_start(rows[:], wgt.rearrange("p (h e) -> (p h) e", e=512)[0:256:17])
-        nc.sync.dma_start(xs[0][:], planes[0])
+        nc.sync.dma_start(planes[0][:], plane_rows[0])
         nc.sync.dma_start(offsets[:], offs)
-        for i in range(1, PACK):
-            nc.sync.dma_start(xs[i][:], planes[i])
-            for q in ((0, 1), (2,), (3,))[i - 1]:
-                load_scales(nc.sync, r8s, r8_scales, q)
+        for i, quadrants in ((1, (0, 1)), (2, (2,)), (3, (3,))):
+            nc.sync.dma_start(planes[i][:], plane_rows[i])
+            for q in quadrants:
+                load_scales(r8s, r8_scales, q)
         nc.sync.dma_start(w4[:].bitcast(I32), w4_words[0].bitcast(I32))
         nc.sync.dma_start(r8[:].bitcast(I32), r8_words[0].rearrange("p n t -> p (n t)").bitcast(I32))
         for q in range(4):
-            load_scales(nc.sync, w4s, w4_scales, q)
+            load_scales(w4s, w4_scales, q)
 
         for a in (0, 32):
             nc.vector.transpose(turned[:, a : a + 32], rows[:, a : a + 32])
-        by_block = turned[:].rearrange("p (c b) -> p b c", b=16)
-        for a, copy in ((0, nc.vector.tensor_copy), (512, nc.scalar.copy)):
+        by_block = turned[:].rearrange("p (g b) -> p b g", b=16)
+        for a, copy in ((0, on_vector), (512, on_scalar)):
             copy(
-                spread[:, a : a + 512].rearrange("p (b c r) -> p b c r", c=4, r=16),
+                spread[:, a : a + 512].rearrange("p (b g r) -> p b g r", g=4, r=16),
                 by_block[:, a // 64 : a // 64 + 8, :].unsqueeze(3).broadcast_to([P, 8, 4, 16]),
             )
         for a in (0, 512):
             nc.vector.transpose(weight[:, a : a + 512], spread[:, a : a + 512])
 
-
         def gather(dst, i, a, b):
-            nc.vector.tensor_tensor(dst, xs[i][:].indirect(offsets[:, a // 16 : b // 16]), weight[:, a:b], MULT)
-
-        def interleave(copy, src, h, a, b):
-            copy(xb[:, a:b, 2 * h : 2 * h + 2], src.rearrange("p t n -> p n t"))
-
-        def interleave_by_fours(copy, src, h, a, b):
-            copy(
-                xb[:, a:b, 2 * h : 2 * h + 2].rearrange("p (c i) t -> p c t i", i=4),
-                src.rearrange("p t (c i) -> p c t i", i=4),
-            )
+            nc.vector.tensor_tensor(dst, planes[i][:].indirect(offsets[:, a // 16 : b // 16]), weight[:, a:b], MULT)
 
         gather(early[:, 0, :], 0, 0, S)
-        for a, b in PIECES:
+        for (a, b, zone), part in zip(pieces, xb_parts):
             gather(early[:, 1, a:b], 1, a, b)
-            interleave_by_fours(nc.scalar.copy, early[:, :, a:b], 0, a, b)
+            on_scalar(
+                part[:, :, 0:2].rearrange("p (c n) t -> p c t n", n=4),
+                early[:, :, a:b].rearrange("p t (c n) -> p c t n", n=4),
+            )
+
+        strip = {}
+
+        def gather_chunks(i, first, n, at):
+            for c in range(n):
+                strip[i, first + c] = at + c
+            gather(late[:, at : at + n, :].rearrange("p r n -> p (r n)"), i, CHUNK * first, CHUNK * (first + n))
+
+        def xb(c):
+            n = int(CHUNK * c >= FIRST_PIECE)
+            a = CHUNK * c - pieces[n][0]
+            return xb_parts[n][:, a : a + CHUNK, :]
+
+        def interleave(c):
+            lo, hi = strip[2, c], strip[3, c]
+            copy = on_scalar if c < SCALAR_CHUNKS else on_vector
+            copy(xb(c)[:, :, 2:4], late[:, lo : hi + 1 : hi - lo, :].rearrange("p t n -> p n t"))
+
+        def quantize(c):
+            cols = slice(CHUNK * c, CHUNK * (c + 1))
+            nc.vector.quantize_mx(
+                out=codes[:, cols].bitcast(FP8X4),
+                scales=scales[:, cols],
+                in_=xb(c).rearrange("p n t -> p (n t)"),
+            )
+
         def multiply(acc, m, first, n):
             for c in range(n):
                 cols = slice(CHUNK * (first + c), CHUNK * (first + c + 1))
                 nc.tensor.matmul_mx(
                     out=acc[:, CHUNK * c : CHUNK * (c + 1)],
-                    lhsT=w4[:, 256 * m : 256 * m + 256].bitcast(FP4X4),
-                    lhsT_scale=w4s[:, 128 * m : 128 * m + 128],
+                    lhsT=w4[:, 2 * P * m : 2 * P * (m + 1)].bitcast(FP4X4),
+                    lhsT_scale=w4s[:, P * m : P * (m + 1)],
                     rhs=codes[:, cols].bitcast(FP8X4),
                     rhs_scale=scales[:, cols],
                     start=c == 0,
@@ -111,103 +163,51 @@ def tile_list_heads_none_kernel(
             cols = slice(CHUNK * first, CHUNK * (first + n))
             nc.tensor.matmul_mx(
                 out=acc,
-                lhsT=r8[:, 128 * m : 128 * m + 128].bitcast(FP8X4),
-                lhsT_scale=r8s[:, 128 * m : 128 * m + 128],
+                lhsT=r8[:, P * m : P * (m + 1)].bitcast(FP8X4),
+                lhsT_scale=r8s[:, P * m : P * (m + 1)],
                 rhs=codes[:, cols].bitcast(FP8X4),
                 rhs_scale=scales[:, cols],
                 start=False,
                 stop=True,
             )
 
-        row = {}
+        def bank(b, width):
+            return psum.tile([P, width], F32, name=f"bank{b}")[:]
 
-        def late_gather(plane, first, n, at):
-            for c in range(n):
-                row[plane, first + c] = at + c
-            gather(late[:, at : at + n, :].rearrange("p r n -> p (r n)"), plane, CHUNK * first, CHUNK * (first + n))
+        def store(pair, m):
+            nc.sync.dma_start(out_halves[:, m, PAIR * pair : PAIR * (pair + 1)], results[HALVES * pair + m][:])
 
-        def weave(copy, c):
-            lo, hi = row[2, c], row[3, c]
-            interleave(copy, late[:, lo : hi + 1 : hi - lo, :], 1, CHUNK * c, CHUNK * (c + 1))
+        gather_chunks(2, 0, EARLY_CHUNKS, 0)
+        gather_chunks(3, 0, FIRST_GATHERS[0], strips - 1)
+        gather_chunks(3, 1, FIRST_GATHERS[1], EARLY_CHUNKS)
+        gather_chunks(3, 2, FIRST_GATHERS[2], EARLY_CHUNKS + 1)
 
-        def quantize(c):
-            cols = slice(CHUNK * c, CHUNK * (c + 1))
-            nc.vector.quantize_mx(
-                out=codes[:, cols].bitcast(FP8X4),
-                scales=scales[:, cols],
-                in_=xb[:, cols, :].rearrange("p n t -> p (n t)"),
-            )
+        last_pair = CHUNKS // 2 - 1
+        sums = []
+        for c in range(CHUNKS):
+            pair, second = divmod(c, 2)
+            interleave(c)
+            if pair > 0 and not second:
+                for m in range(HALVES):
+                    on_scalar(results[HALVES * (pair - 1) + m][:], sums[m])
+                    store(pair - 1, m)
+            quantize(c)
+            if c in HELD_GATHERS:
+                i, first = HELD_GATHERS[c]
+                gather_chunks(i, first, 2, strip[i, c] - 1)
+            if pair < HALF_BY_HALF_PAIR:
+                if not second:
+                    sums = [bank(HALVES * pair + m, PAIR) for m in range(HALVES)]
+                for m in range(HALVES):
+                    multiply(sums[m][:, CHUNK * second : CHUNK * (second + 1)], m, c, 1)
+            elif pair < last_pair and second:
+                sums = [bank(HALVES * pair + m, PAIR) for m in range(HALVES)]
+                for m in range(HALVES):
+                    multiply(sums[m], m, c - 1, 2)
 
-        def product(first, n, banks):
-            if len(banks) == 2:
-                halves = [psum.tile([P, n * CHUNK], F32, name=f"acc{b}")[:] for b in banks]
-                whole = None
-            else:
-                whole = psum.tile([P, 2, n * CHUNK], F32, name=f"acc{banks[0]}")
-                halves = [whole[:, m, :] for m in range(2)]
-            for m in range(2):
-                multiply(halves[m], m, first, n)
-            return first, n, halves, whole
-
-        def empty(group, copies, split):
-            first, n, halves, whole = group
-            cols = slice(CHUNK * first, CHUNK * (first + n))
-            res = keep.tile([P, 2, n * CHUNK], F32, name=f"res{first}", align_bytes=64, offset=32768 + 1024 * first)
-            if whole is not None:
-                copies[0](res[:], whole[:])
-            else:
-                for m in range(2):
-                    copies[m](res[:, m, :], halves[m])
-                    if split:
-                        nc.sync.dma_start(out_halves[:, m, cols], res[:, m, :])
-            if not split:
-                nc.sync.dma_start(out_halves[:, :, cols], res[:])
-
-        act, dve = nc.scalar.copy, nc.vector.tensor_copy
-
-        def product_by_chunks(halves, first, c):
-            for m in range(2):
-                multiply(halves[m][:, CHUNK * c : CHUNK * (c + 1)], m, first + c, 1)
-
-        def banks_of(banks, n):
-            return [psum.tile([P, n * CHUNK], F32, name=f"acc{b}")[:] for b in banks]
-
-        late_gather(2, 0, 6, 0)
-        late_gather(3, 0, 1, 9)
-        late_gather(3, 1, 1, 6)
-        late_gather(3, 2, 2, 7)
-        weave(act, 0)
-        quantize(0)
-        late_gather(3, 4, 2, 9)
-        h0 = banks_of((0, 1), 2)
-        product_by_chunks(h0, 0, 0)
-        weave(act, 1)
-        quantize(1)
-        product_by_chunks(h0, 0, 1)
-        weave(act, 2)
-        empty((0, 2, h0, None), (act, act), True)
-        quantize(2)
-        late_gather(3, 6, 2, 6)
-        h2 = banks_of((2, 3), 2)
-        product_by_chunks(h2, 2, 0)
-        weave(act, 3)
-        quantize(3)
-        late_gather(2, 6, 2, 2)
-        product_by_chunks(h2, 2, 1)
-        weave(act, 4)
-        empty((2, 2, h2, None), (act, act), True)
-        quantize(4)
-        weave(act, 5)
-        quantize(5)
-        g4 = product(4, 2, (4, 5))
-        weave(dve, 6)
-        empty(g4, (act, act), True)
-        quantize(6)
-        weave(dve, 7)
-        quantize(7)
-        res6 = keep.tile([P, 2, 2 * CHUNK], F32, name="res6", align_bytes=64, offset=38912)
-        for m, (copy, banks) in enumerate(((dve, (6, 7)), (act, (0, 1)))):
-            for c, acc in enumerate(banks_of(banks, 1)):
-                multiply(acc, m, 6 + c, 1)
-                copy(res6[:, m, CHUNK * c : CHUNK * (c + 1)], acc)
-            nc.sync.dma_start(out_halves[:, m, 6 * CHUNK :], res6[:, m, :])
+        for m, (copy, banks) in enumerate(((on_vector, (6, 7)), (on_scalar, (0, 1)))):
+            for c, b in enumerate(banks):
+                acc = bank(b, CHUNK)
+                multiply(acc, m, 2 * last_pair + c, 1)
+                copy(results[HALVES * last_pair + m][:, CHUNK * c : CHUNK * (c + 1)], acc)
+            store(last_pair, m)

@@ -31,7 +31,7 @@ HALF_BY_HALF_PAIR = 2
 
 KIB = 1024
 ZONE = 32 * KIB
-RESERVED = 16 * KIB
+RESERVED = 17 * KIB
 WEIGHT_ZONE, EARLY_ZONE, LATE_ZONE, WOVEN_ZONE, CODES_ZONE, SPARE_ZONE = 0, 3, 4, 5, 6, 7
 PLANE_ZONES = (1, 2)
 RESULT_ZONES = (SPARE_ZONE, EARLY_ZONE, PLANE_ZONES[1], PLANE_ZONES[0])
@@ -46,8 +46,8 @@ def tile_list_heads_none_kernel(
     on_scalar, on_vector = nc.scalar.copy, nc.vector.tensor_copy
 
     with ExitStack() as ctx:
-        lists = ctx.enter_context(tc.tile_pool(name="lists", bufs=1))
         keep = ctx.enter_context(tc.tile_pool(name="keep", bufs=1))
+        lists = ctx.enter_context(tc.tile_pool(name="lists", bufs=1))
         psum = ctx.enter_context(tc.psum_pool(name="psum", bufs=1))
 
         filled = {}
@@ -57,9 +57,9 @@ def tile_list_heads_none_kernel(
             size = itemsize
             for n in shape[1:]:
                 size = size * n
-            filled[zone] = used + size
+            filled[zone] = used + (size + KIB - 1) // KIB * KIB
             start = max(zone * ZONE - RESERVED, 0)
-            return keep.tile(shape, dtype, name=name, align_bytes=64, offset=start + used)
+            return keep.tile(shape, dtype, name=name, align_bytes=KIB, offset=start + used)
 
         offsets = lists.tile([P, S // 16], U16, name="offsets")
         weight = place("weight", [P, S], F32, 4, WEIGHT_ZONE)

@@ -22,26 +22,23 @@ CHUNK = 128
 CHUNKS = S // CHUNK
 PAIR = 2 * CHUNK
 
-FIRST_PIECE = 384
-EARLY_CHUNKS = 6
+EARLY = 736
 SCALAR_CHUNKS = 6
-FIRST_GATHERS = (1, 1, 2)
-HELD_GATHERS = {0: (3, 4), 2: (3, 6), 3: (2, 6)}
 HALF_BY_HALF_PAIR = 2
 
 KIB = 1024
 ZONE = 32 * KIB
 RESERVED = 17 * KIB
-WEIGHT_ZONE, EARLY_ZONE, LATE_ZONE, WOVEN_ZONE, CODES_ZONE, SPARE_ZONE = 0, 3, 4, 5, 6, 7
-PLANE_ZONES = (1, 2)
-RESULT_ZONES = (SPARE_ZONE, EARLY_ZONE, PLANE_ZONES[1], PLANE_ZONES[0])
+WEIGHT_ZONE, FIRST_ZONE, RING_ZONE, WOVEN_ZONE, CODES_ZONE, SPARE_ZONE = 0, 3, 4, 5, 6, 7
+PLANE_ZONES = (2, 1)
+RESULT_ZONES = (SPARE_ZONE, FIRST_ZONE, PLANE_ZONES[0], PLANE_ZONES[1])
 
 
 def tile_list_heads_none_kernel(
     tc, xT, w4_words, w4_scales, r8_words, r8_scales, wgt, offs, out
 ):
     nc = tc.nc
-    plane_rows = xT.rearrange("(p i) t -> i p t", i=PACK)
+    plane_rows = xT.rearrange("(p t) n -> t p n", t=PACK)
     out_halves = out.rearrange("(m p) j -> p m j", p=P)
     on_scalar, on_vector = nc.scalar.copy, nc.vector.tensor_copy
 
@@ -66,16 +63,14 @@ def tile_list_heads_none_kernel(
         rows = place("rows", [P, 64], F32, 4, WEIGHT_ZONE)
         turned = place("turned", [P, 64], F32, 4, WEIGHT_ZONE)
         spread = place("spread", [P, S], F32, 4, WEIGHT_ZONE)
-        planes = [place(f"plane{i}", [P, T], F32, 4, PLANE_ZONES[i % 2]) for i in range(PACK)]
-        early = place("early", [P, 2, S], F32, 4, EARLY_ZONE)
-        w4 = place("w4", [P, 2 * M], U8, 1, EARLY_ZONE)
-        r8 = place("r8", [P, M], U32, 4, EARLY_ZONE)
-        w4s = place("w4s", [P, M], U8, 1, EARLY_ZONE)
-        r8s = place("r8s", [P, M], U8, 1, EARLY_ZONE)
-        strips = EARLY_CHUNKS + sum(FIRST_GATHERS) + 1
-        late = place("late", [P, strips, CHUNK], F32, 4, LATE_ZONE)
-        pieces = ((0, FIRST_PIECE, SPARE_ZONE), (FIRST_PIECE, S, WOVEN_ZONE))
-        xb_parts = [place(f"xb{a}", [P, b - a, PACK], BF16, 2, zone) for a, b, zone in pieces]
+        planes = [place(f"plane{t}", [P, T], F32, 4, PLANE_ZONES[t % 2]) for t in range(PACK)]
+        first = place("first", [P, S], F32, 4, FIRST_ZONE)
+        w4 = place("w4", [P, 2 * M], U8, 1, FIRST_ZONE)
+        r8 = place("r8", [P, M], U32, 4, FIRST_ZONE)
+        w4s = place("w4s", [P, M], U8, 1, FIRST_ZONE)
+        r8s = place("r8s", [P, M], U8, 1, FIRST_ZONE)
+        ring = place("ring", [P, S - CHUNK + 3 * EARLY], F32, 4, RING_ZONE)
+        xb = place("xb", [P, S, PACK], BF16, 2, WOVEN_ZONE)
         codes = place("codes", [P, S], U32, 4, CODES_ZONE)
         scales = place("scales", [P, S], U8, 1, CODES_ZONE)
         results = [
@@ -90,10 +85,10 @@ def tile_list_heads_none_kernel(
             nc.sync.dma_start(tile[32 * q : 32 * q + 4, :].bitcast(I32), src[0, 4 * q : 4 * q + 4, :].bitcast(I32))
 
         nc.sync.dma_start(rows[:], wgt.rearrange("p (h e) -> (p h) e", e=512)[0:256:17])
-        nc.sync.dma_start(planes[0][:], plane_rows[0])
+        nc.sync.dma_start(planes[3][:], plane_rows[3])
         nc.sync.dma_start(offsets[:], offs)
-        for i, quadrants in ((1, (0, 1)), (2, (2,)), (3, (3,))):
-            nc.sync.dma_start(planes[i][:], plane_rows[i])
+        for t, quadrants in ((2, (0, 1)), (1, (2,)), (0, (3,))):
+            nc.sync.dma_start(planes[t][:], plane_rows[t])
             for q in quadrants:
                 load_scales(r8s, r8_scales, q)
         nc.sync.dma_start(w4[:].bitcast(I32), w4_words[0].bitcast(I32))
@@ -112,45 +107,29 @@ def tile_list_heads_none_kernel(
         for a in (0, 512):
             nc.vector.transpose(weight[:, a : a + 512], spread[:, a : a + 512])
 
-        def gather(dst, i, a, b):
-            nc.vector.tensor_tensor(dst, planes[i][:].indirect(offsets[:, a // 16 : b // 16]), weight[:, a:b], MULT)
+        def gather(dst, t, a, b):
+            nc.vector.tensor_tensor(dst, planes[t][:].indirect(offsets[:, a // 16 : b // 16]), weight[:, a:b], MULT)
 
-        gather(early[:, 0, :], 0, 0, S)
-        for (a, b, zone), part in zip(pieces, xb_parts):
-            gather(early[:, 1, a:b], 1, a, b)
-            on_scalar(
-                part[:, :, 0:2].rearrange("p (c n) t -> p c t n", n=4),
-                early[:, :, a:b].rearrange("p t (c n) -> p c t n", n=4),
-            )
-
-        strip = {}
-
-        def gather_chunks(i, first, n, at):
-            for c in range(n):
-                strip[i, first + c] = at + c
-            gather(late[:, at : at + n, :].rearrange("p r n -> p (r n)"), i, CHUNK * first, CHUNK * (first + n))
-
-        def xb(c):
-            n = int(CHUNK * c >= FIRST_PIECE)
-            a = CHUNK * c - pieces[n][0]
-            return xb_parts[n][:, a : a + CHUNK, :]
+        def gather_to_ring(t, a, b):
+            gather(ring[:, EARLY * t + a : EARLY * t + b], t, a, b)
 
         def interleave(c):
-            lo, hi = strip[2, c], strip[3, c]
+            a = CHUNK * c
+            three = ring[:, a : a + 3 * EARLY].rearrange("p (t e) -> p t e", t=3)[:, :, 0:CHUNK]
             copy = on_scalar if c < SCALAR_CHUNKS else on_vector
-            copy(xb(c)[:, :, 2:4], late[:, lo : hi + 1 : hi - lo, :].rearrange("p t n -> p n t"))
+            copy(xb[:, a : a + CHUNK, 0:3], three.rearrange("p t n -> p n t"))
 
         def quantize(c):
             cols = slice(CHUNK * c, CHUNK * (c + 1))
             nc.vector.quantize_mx(
                 out=codes[:, cols].bitcast(FP8X4),
                 scales=scales[:, cols],
-                in_=xb(c).rearrange("p n t -> p (n t)"),
+                in_=xb[:, cols, :].rearrange("p n t -> p (n t)"),
             )
 
-        def multiply(acc, m, first, n):
+        def multiply(acc, m, first_chunk, n):
             for c in range(n):
-                cols = slice(CHUNK * (first + c), CHUNK * (first + c + 1))
+                cols = slice(CHUNK * (first_chunk + c), CHUNK * (first_chunk + c + 1))
                 nc.tensor.matmul_mx(
                     out=acc[:, CHUNK * c : CHUNK * (c + 1)],
                     lhsT=w4[:, 2 * P * m : 2 * P * (m + 1)].bitcast(FP4X4),
@@ -160,7 +139,7 @@ def tile_list_heads_none_kernel(
                     start=c == 0,
                     stop=False,
                 )
-            cols = slice(CHUNK * first, CHUNK * (first + n))
+            cols = slice(CHUNK * first_chunk, CHUNK * (first_chunk + n))
             nc.tensor.matmul_mx(
                 out=acc,
                 lhsT=r8[:, P * m : P * (m + 1)].bitcast(FP8X4),
@@ -177,10 +156,13 @@ def tile_list_heads_none_kernel(
         def store(pair, m):
             nc.sync.dma_start(out_halves[:, m, PAIR * pair : PAIR * (pair + 1)], results[HALVES * pair + m][:])
 
-        gather_chunks(2, 0, EARLY_CHUNKS, 0)
-        gather_chunks(3, 0, FIRST_GATHERS[0], strips - 1)
-        gather_chunks(3, 1, FIRST_GATHERS[1], EARLY_CHUNKS)
-        gather_chunks(3, 2, FIRST_GATHERS[2], EARLY_CHUNKS + 1)
+        gather(first[:], 3, 0, S)
+        on_scalar(xb[:, :, 3], first[:])
+        gather_to_ring(2, 0, S)
+        gather_to_ring(1, 0, EARLY)
+        for a, b in ((0, 1), (1, 2), (2, 4)):
+            gather_to_ring(0, CHUNK * a, CHUNK * b)
+        held = {0: (0, 4 * CHUNK, 6 * CHUNK), 2: (1, EARLY, S), 3: (0, 6 * CHUNK, S)}
 
         last_pair = CHUNKS // 2 - 1
         sums = []
@@ -192,9 +174,8 @@ def tile_list_heads_none_kernel(
                     on_scalar(results[HALVES * (pair - 1) + m][:], sums[m])
                     store(pair - 1, m)
             quantize(c)
-            if c in HELD_GATHERS:
-                i, first = HELD_GATHERS[c]
-                gather_chunks(i, first, 2, strip[i, c] - 1)
+            if c in held:
+                gather_to_ring(*held[c])
             if pair < HALF_BY_HALF_PAIR:
                 if not second:
                     sums = [bank(HALVES * pair + m, PAIR) for m in range(HALVES)]

@@ -22,23 +22,26 @@ CHUNK = 128
 CHUNKS = S // CHUNK
 PAIR = 2 * CHUNK
 
-EARLY = 736
+PAIRED_CHUNKS = 5
+EARLY_CHUNKS = 6
 SCALAR_CHUNKS = 6
+FIRST_GATHERS = (1, 1, 2)
+HELD_GATHERS = {0: (3, 4), 2: (3, 6), 3: (2, 6)}
 HALF_BY_HALF_PAIR = 2
 
 KIB = 1024
 ZONE = 32 * KIB
 RESERVED = 17 * KIB
-WEIGHT_ZONE, FIRST_ZONE, RING_ZONE, WOVEN_ZONE, CODES_ZONE, SPARE_ZONE = 0, 3, 4, 5, 6, 7
-PLANE_ZONES = (2, 1)
-RESULT_ZONES = (SPARE_ZONE, FIRST_ZONE, PLANE_ZONES[0], PLANE_ZONES[1])
+WEIGHT_ZONE, EARLY_ZONE, LATE_ZONE, WOVEN_ZONE, CODES_ZONE, SPARE_ZONE = 0, 3, 4, 5, 6, 7
+PLANE_ZONES = (1, 2)
+RESULT_ZONES = (SPARE_ZONE, EARLY_ZONE, PLANE_ZONES[1], PLANE_ZONES[0])
 
 
 def tile_list_heads_none_kernel(
     tc, xT, w4_words, w4_scales, r8_words, r8_scales, wgt, offs, out
 ):
     nc = tc.nc
-    plane_rows = xT.rearrange("(p t) n -> t p n", t=PACK)
+    plane_rows = xT.rearrange("(p i) t -> i p t", i=PACK)
     out_halves = out.rearrange("(m p) j -> p m j", p=P)
     on_scalar, on_vector = nc.scalar.copy, nc.vector.tensor_copy
 
@@ -63,14 +66,18 @@ def tile_list_heads_none_kernel(
         rows = place("rows", [P, 64], F32, 4, WEIGHT_ZONE)
         turned = place("turned", [P, 64], F32, 4, WEIGHT_ZONE)
         spread = place("spread", [P, S], F32, 4, WEIGHT_ZONE)
-        planes = [place(f"plane{t}", [P, T], F32, 4, PLANE_ZONES[t % 2]) for t in range(PACK)]
-        first = place("first", [P, S], F32, 4, FIRST_ZONE)
-        w4 = place("w4", [P, 2 * M], U8, 1, FIRST_ZONE)
-        r8 = place("r8", [P, M], U32, 4, FIRST_ZONE)
-        w4s = place("w4s", [P, M], U8, 1, FIRST_ZONE)
-        r8s = place("r8s", [P, M], U8, 1, FIRST_ZONE)
-        ring = place("ring", [P, S - CHUNK + 3 * EARLY], F32, 4, RING_ZONE)
-        xb = place("xb", [P, S, PACK], BF16, 2, WOVEN_ZONE)
+        planes = [place(f"plane{i}", [P, T], F32, 4, PLANE_ZONES[i % 2]) for i in range(PACK)]
+        w4 = place("w4", [P, 2 * M], U8, 1, EARLY_ZONE)
+        r8 = place("r8", [P, M], U32, 4, EARLY_ZONE)
+        w4s = place("w4s", [P, M], U8, 1, EARLY_ZONE)
+        r8s = place("r8s", [P, M], U8, 1, EARLY_ZONE)
+        plane2_at = 2 * CHUNKS
+        strips = 2 * (plane2_at + 5) - (CHUNKS + 5) + 1
+        picked_at = LATE_ZONE * ZONE - RESERVED - plane2_at * CHUNK * 4
+        picked = keep.tile([P, strips, CHUNK], F32, name="picked", align_bytes=KIB, offset=picked_at)
+        cut = CHUNK * PAIRED_CHUNKS
+        pieces = ((0, cut, SPARE_ZONE), (cut, S, WOVEN_ZONE))
+        xb_parts = [place(f"xb{a}", [P, b - a, PACK], BF16, 2, zone) for a, b, zone in pieces]
         codes = place("codes", [P, S], U32, 4, CODES_ZONE)
         scales = place("scales", [P, S], U8, 1, CODES_ZONE)
         results = [
@@ -85,10 +92,10 @@ def tile_list_heads_none_kernel(
             nc.sync.dma_start(tile[32 * q : 32 * q + 4, :].bitcast(I32), src[0, 4 * q : 4 * q + 4, :].bitcast(I32))
 
         nc.sync.dma_start(rows[:], wgt.rearrange("p (h e) -> (p h) e", e=512)[0:256:17])
-        nc.sync.dma_start(planes[3][:], plane_rows[3])
+        nc.sync.dma_start(planes[0][:], plane_rows[0])
         nc.sync.dma_start(offsets[:], offs)
-        for t, quadrants in ((2, (0, 1)), (1, (2,)), (0, (3,))):
-            nc.sync.dma_start(planes[t][:], plane_rows[t])
+        for i, quadrants in ((1, (0, 1)), (2, (2,)), (3, (3,))):
+            nc.sync.dma_start(planes[i][:], plane_rows[i])
             for q in quadrants:
                 load_scales(r8s, r8_scales, q)
         nc.sync.dma_start(w4[:].bitcast(I32), w4_words[0].bitcast(I32))
@@ -107,29 +114,53 @@ def tile_list_heads_none_kernel(
         for a in (0, 512):
             nc.vector.transpose(weight[:, a : a + 512], spread[:, a : a + 512])
 
-        def gather(dst, t, a, b):
-            nc.vector.tensor_tensor(dst, planes[t][:].indirect(offsets[:, a // 16 : b // 16]), weight[:, a:b], MULT)
+        def gather(dst, i, a, b):
+            nc.vector.tensor_tensor(dst, planes[i][:].indirect(offsets[:, a // 16 : b // 16]), weight[:, a:b], MULT)
 
-        def gather_to_ring(t, a, b):
-            gather(ring[:, EARLY * t + a : EARLY * t + b], t, a, b)
+        strip = {}
+
+        def gather_chunks(i, first, n, at):
+            for c in range(n):
+                strip[i, first + c] = at + c
+            gather(picked[:, at : at + n, :].rearrange("p r n -> p (r n)"), i, CHUNK * first, CHUNK * (first + n))
+
+        def xb(c):
+            n = int(c >= PAIRED_CHUNKS)
+            a = CHUNK * c - pieces[n][0]
+            return xb_parts[n][:, a : a + CHUNK, :]
 
         def interleave(c):
-            a = CHUNK * c
-            three = ring[:, a : a + 3 * EARLY].rearrange("p (t e) -> p t e", t=3)[:, :, 0:CHUNK]
-            copy = on_scalar if c < SCALAR_CHUNKS else on_vector
-            copy(xb[:, a : a + CHUNK, 0:3], three.rearrange("p t n -> p n t"))
+            i = 2 if c < PAIRED_CHUNKS else 1
+            lo, hi = strip[i, c], strip[3, c]
+            src = picked[:, lo : hi + 1 : hi - strip[2, c], :]
+            if c < SCALAR_CHUNKS:
+                on_scalar(xb(c)[:, :, i:PACK], src.rearrange("p t n -> p n t"))
+            else:
+                on_vector(
+                    xb(c)[:, :, i:PACK].rearrange("p (c n) t -> p c t n", n=2),
+                    src.rearrange("p t (c n) -> p c t n", n=2),
+                )
+
+        early = picked[:, 0:plane2_at, :].rearrange("p (t r) n -> p t (r n)", t=2)
+        gather_chunks(0, 0, CHUNKS, 0)
+        on_scalar(xb_parts[1][:, :, 0], early[:, 0, cut:S])
+        gather_chunks(1, 0, CHUNKS, CHUNKS)
+        on_scalar(
+            xb_parts[0][:, :, 0:2].rearrange("p (c n) t -> p c t n", n=4),
+            early[:, :, 0:cut].rearrange("p t (c n) -> p c t n", n=4),
+        )
 
         def quantize(c):
             cols = slice(CHUNK * c, CHUNK * (c + 1))
             nc.vector.quantize_mx(
                 out=codes[:, cols].bitcast(FP8X4),
                 scales=scales[:, cols],
-                in_=xb[:, cols, :].rearrange("p n t -> p (n t)"),
+                in_=xb(c).rearrange("p n t -> p (n t)"),
             )
 
-        def multiply(acc, m, first_chunk, n):
+        def multiply(acc, m, first, n):
             for c in range(n):
-                cols = slice(CHUNK * (first_chunk + c), CHUNK * (first_chunk + c + 1))
+                cols = slice(CHUNK * (first + c), CHUNK * (first + c + 1))
                 nc.tensor.matmul_mx(
                     out=acc[:, CHUNK * c : CHUNK * (c + 1)],
                     lhsT=w4[:, 2 * P * m : 2 * P * (m + 1)].bitcast(FP4X4),
@@ -139,7 +170,7 @@ def tile_list_heads_none_kernel(
                     start=c == 0,
                     stop=False,
                 )
-            cols = slice(CHUNK * first_chunk, CHUNK * (first_chunk + n))
+            cols = slice(CHUNK * first, CHUNK * (first + n))
             nc.tensor.matmul_mx(
                 out=acc,
                 lhsT=r8[:, P * m : P * (m + 1)].bitcast(FP8X4),
@@ -156,13 +187,10 @@ def tile_list_heads_none_kernel(
         def store(pair, m):
             nc.sync.dma_start(out_halves[:, m, PAIR * pair : PAIR * (pair + 1)], results[HALVES * pair + m][:])
 
-        gather(first[:], 3, 0, S)
-        on_scalar(xb[:, :, 3], first[:])
-        gather_to_ring(2, 0, S)
-        gather_to_ring(1, 0, EARLY)
-        for a, b in ((0, 1), (1, 2), (2, 4)):
-            gather_to_ring(0, CHUNK * a, CHUNK * b)
-        held = {0: (0, 4 * CHUNK, 6 * CHUNK), 2: (1, EARLY, S), 3: (0, 6 * CHUNK, S)}
+        gather_chunks(2, 0, EARLY_CHUNKS, plane2_at)
+        gather_chunks(3, 0, FIRST_GATHERS[0], strips - 1)
+        gather_chunks(3, 1, FIRST_GATHERS[1], plane2_at + EARLY_CHUNKS)
+        gather_chunks(3, 2, FIRST_GATHERS[2], plane2_at + EARLY_CHUNKS + 1)
 
         last_pair = CHUNKS // 2 - 1
         sums = []
@@ -174,8 +202,9 @@ def tile_list_heads_none_kernel(
                     on_scalar(results[HALVES * (pair - 1) + m][:], sums[m])
                     store(pair - 1, m)
             quantize(c)
-            if c in held:
-                gather_to_ring(*held[c])
+            if c in HELD_GATHERS:
+                i, first = HELD_GATHERS[c]
+                gather_chunks(i, first, 2, strip[i, c] - 1)
             if pair < HALF_BY_HALF_PAIR:
                 if not second:
                     sums = [bank(HALVES * pair + m, PAIR) for m in range(HALVES)]

@@ -159,27 +159,21 @@ def tile_list_heads_none_kernel(
             )
 
         def multiply(acc, m, first, n):
-            for c in range(n):
-                cols = slice(CHUNK * (first + c), CHUNK * (first + c + 1))
+            cols = slice(CHUNK * first, CHUNK * (first + n))
+            stationary = (
+                (w4[:, 2 * P * m : 2 * P * (m + 1)].bitcast(FP4X4), w4s),
+                (r8[:, P * m : P * (m + 1)].bitcast(FP8X4), r8s),
+            )
+            for t, (words, plane) in enumerate(stationary):
                 nc.tensor.matmul_mx(
-                    out=acc[:, CHUNK * c : CHUNK * (c + 1)],
-                    lhsT=w4[:, 2 * P * m : 2 * P * (m + 1)].bitcast(FP4X4),
-                    lhsT_scale=w4s[:, P * m : P * (m + 1)],
+                    out=acc,
+                    lhsT=words,
+                    lhsT_scale=plane[:, P * m : P * (m + 1)],
                     rhs=codes[:, cols].bitcast(FP8X4),
                     rhs_scale=scales[:, cols],
-                    start=c == 0,
-                    stop=False,
+                    start=t == 0,
+                    stop=t == 1,
                 )
-            cols = slice(CHUNK * first, CHUNK * (first + n))
-            nc.tensor.matmul_mx(
-                out=acc,
-                lhsT=r8[:, P * m : P * (m + 1)].bitcast(FP8X4),
-                lhsT_scale=r8s[:, P * m : P * (m + 1)],
-                rhs=codes[:, cols].bitcast(FP8X4),
-                rhs_scale=scales[:, cols],
-                start=False,
-                stop=True,
-            )
 
         def bank(b, width):
             return psum.tile([P, width], F32, name=f"bank{b}")[:]
@@ -210,10 +204,12 @@ def tile_list_heads_none_kernel(
                     sums = [bank(HALVES * pair + m, PAIR) for m in range(HALVES)]
                 for m in range(HALVES):
                     multiply(sums[m][:, CHUNK * second : CHUNK * (second + 1)], m, c, 1)
-            elif pair < last_pair and second:
-                sums = [bank(HALVES * pair + m, PAIR) for m in range(HALVES)]
-                for m in range(HALVES):
-                    multiply(sums[m], m, c - 1, 2)
+            elif pair < last_pair:
+                if not second:
+                    sums = [bank(HALVES * pair + m, PAIR) for m in range(HALVES)]
+                multiply(sums[0][:, CHUNK * second : CHUNK * (second + 1)], 0, c, 1)
+                if second:
+                    multiply(sums[1], 1, c - 1, 2)
 
         for m, (copy, banks) in enumerate(((on_vector, (6, 7)), (on_scalar, (0, 1)))):
             for c, b in enumerate(banks):

@@ -21,13 +21,9 @@ HALVES = M // P
 CHUNK = 128
 CHUNKS = S // CHUNK
 PAIR = 2 * CHUNK
+PAIRS = S // PAIR
 
-PAIRED_CHUNKS = 5
-EARLY_CHUNKS = 6
-SCALAR_CHUNKS = 6
-FIRST_GATHERS = (1, 1, 2)
-HELD_GATHERS = {0: (3, 4), 2: (3, 6), 3: (2, 6)}
-HALF_BY_HALF_PAIR = 2
+EARLY_PAIRS = 3
 
 KIB = 1024
 ZONE = 32 * KIB
@@ -71,13 +67,9 @@ def tile_list_heads_none_kernel(
         r8 = place("r8", [P, M], U32, 4, EARLY_ZONE)
         w4s = place("w4s", [P, M], U8, 1, EARLY_ZONE)
         r8s = place("r8s", [P, M], U8, 1, EARLY_ZONE)
-        plane2_at = 2 * CHUNKS
-        strips = 2 * (plane2_at + 5) - (CHUNKS + 5) + 1
-        picked_at = LATE_ZONE * ZONE - RESERVED - plane2_at * CHUNK * 4
-        picked = keep.tile([P, strips, CHUNK], F32, name="picked", align_bytes=KIB, offset=picked_at)
-        cut = CHUNK * PAIRED_CHUNKS
-        pieces = ((0, cut, SPARE_ZONE), (cut, S, WOVEN_ZONE))
-        xb_parts = [place(f"xb{a}", [P, b - a, PACK], BF16, 2, zone) for a, b, zone in pieces]
+        picked_at = LATE_ZONE * ZONE - RESERVED - 2 * S * 4
+        picked = keep.tile([P, PACK * PAIRS, PAIR], F32, name="picked", align_bytes=KIB, offset=picked_at)
+        woven = place("woven", [P, S, PACK], BF16, 2, WOVEN_ZONE)
         codes = place("codes", [P, S], U32, 4, CODES_ZONE)
         scales = place("scales", [P, S], U8, 1, CODES_ZONE)
         results = [
@@ -117,37 +109,37 @@ def tile_list_heads_none_kernel(
         def gather(dst, i, a, b):
             nc.vector.tensor_tensor(dst, planes[i][:].indirect(offsets[:, a // 16 : b // 16]), weight[:, a:b], MULT)
 
-        strip = {}
+        def home(i, pair):
+            return PAIRS * i + pair
 
-        def gather_chunks(i, first, n, at):
-            for c in range(n):
-                strip[i, first + c] = at + c
-            gather(picked[:, at : at + n, :].rearrange("p r n -> p (r n)"), i, CHUNK * first, CHUNK * (first + n))
+        def gather_pairs(i, first, n, at):
+            gather(picked[:, at : at + n, :].rearrange("p r n -> p (r n)"), i, PAIR * first, PAIR * (first + n))
 
-        def xb(c):
-            n = int(c >= PAIRED_CHUNKS)
-            a = CHUNK * c - pieces[n][0]
-            return xb_parts[n][:, a : a + CHUNK, :]
+        def xb(a, b):
+            return woven[:, a:b, :]
 
-        def interleave(c):
-            i = 2 if c < PAIRED_CHUNKS else 1
-            lo, hi = strip[i, c], strip[3, c]
-            src = picked[:, lo : hi + 1 : hi - strip[2, c], :]
-            if c < SCALAR_CHUNKS:
-                on_scalar(xb(c)[:, :, i:PACK], src.rearrange("p t n -> p n t"))
-            else:
-                on_vector(
-                    xb(c)[:, :, i:PACK].rearrange("p (c n) t -> p c t n", n=2),
-                    src.rearrange("p t (c n) -> p c t n", n=2),
-                )
+        def late_planes(a, b, strips):
+            at = a % PAIR
+            return PACK - len(strips), picked[:, strips.start : strips.stop : strips.step, at : at + b - a]
 
-        early = picked[:, 0:plane2_at, :].rearrange("p (t r) n -> p t (r n)", t=2)
-        gather_chunks(0, 0, CHUNKS, 0)
-        on_scalar(xb_parts[1][:, :, 0], early[:, 0, cut:S])
-        gather_chunks(1, 0, CHUNKS, CHUNKS)
+        def interleave_on_scalar(a, b, strips):
+            i, values = late_planes(a, b, strips)
+            on_scalar(xb(a, b)[:, :, i:PACK], values.rearrange("p t n -> p n t"))
+
+        def interleave_on_vector(a, b, strips):
+            i, values = late_planes(a, b, strips)
+            on_vector(
+                xb(a, b)[:, :, i:PACK].rearrange("p (c n) t -> p c t n", n=2),
+                values.rearrange("p t (c n) -> p c t n", n=2),
+            )
+
+        by_pair = woven[:].rearrange("p (r n) t -> p r n t", n=PAIR)
+        gather_pairs(0, 0, PAIRS, home(0, 0))
+        on_scalar(by_pair[:, 1:PAIRS:2, :, 0], picked[:, 1:PAIRS:2, :])
+        gather_pairs(1, 0, PAIRS, home(1, 0))
         on_scalar(
-            xb_parts[0][:, :, 0:2].rearrange("p (c n) t -> p c t n", n=4),
-            early[:, :, 0:cut].rearrange("p t (c n) -> p c t n", n=4),
+            by_pair[:, 0:PAIRS:2, :, 0:2].rearrange("p r (c n) t -> p r c t n", n=4),
+            picked[:, 0 : 2 * PAIRS : 2, :].rearrange("p (t r) (c n) -> p r c t n", t=2, n=4),
         )
 
         def quantize(c):
@@ -155,7 +147,7 @@ def tile_list_heads_none_kernel(
             nc.vector.quantize_mx(
                 out=codes[:, cols].bitcast(FP8X4),
                 scales=scales[:, cols],
-                in_=xb(c).rearrange("p n t -> p (n t)"),
+                in_=xb(cols.start, cols.stop).rearrange("p n t -> p (n t)"),
             )
 
         def multiply(acc, m, first, n):
@@ -181,36 +173,50 @@ def tile_list_heads_none_kernel(
         def store(pair, m):
             nc.sync.dma_start(out_halves[:, m, PAIR * pair : PAIR * (pair + 1)], results[HALVES * pair + m][:])
 
-        gather_chunks(2, 0, EARLY_CHUNKS, plane2_at)
-        gather_chunks(3, 0, FIRST_GATHERS[0], strips - 1)
-        gather_chunks(3, 1, FIRST_GATHERS[1], plane2_at + EARLY_CHUNKS)
-        gather_chunks(3, 2, FIRST_GATHERS[2], plane2_at + EARLY_CHUNKS + 1)
+        def empty(pair, sums):
+            for m in range(HALVES):
+                on_scalar(results[HALVES * pair + m][:], sums[m])
+                store(pair, m)
 
-        last_pair = CHUNKS // 2 - 1
-        sums = []
-        for c in range(CHUNKS):
-            pair, second = divmod(c, 2)
-            interleave(c)
-            if pair > 0 and not second:
-                for m in range(HALVES):
-                    on_scalar(results[HALVES * (pair - 1) + m][:], sums[m])
-                    store(pair - 1, m)
+        def chunk_of(sums, m, c):
+            return sums[m][:, CHUNK * (c % 2) : CHUNK * (c % 2 + 1)]
+
+        sums = [[bank(HALVES * pair + m, PAIR) for m in range(HALVES)] for pair in range(PAIRS - 1)]
+        gather_pairs(2, 0, EARLY_PAIRS, home(2, 0))
+        last_strips = range(home(1, 3), home(2, 3) + 1, 2)
+        later = (home(3, 2), last_strips[2])
+        for c in range(2):
+            gather(picked[:, later[c], CHUNK * c : CHUNK * (c + 1)], 3, CHUNK * c, CHUNK * (c + 1))
+        gather_pairs(3, 1, 1, home(3, 1))
+        for c in range(2):
+            interleave_on_scalar(CHUNK * c, CHUNK * (c + 1), range(home(2, 0), later[c] + 1, later[c] - home(2, 0)))
             quantize(c)
-            if c in HELD_GATHERS:
-                i, first = HELD_GATHERS[c]
-                gather_chunks(i, first, 2, strip[i, c] - 1)
-            if pair < HALF_BY_HALF_PAIR:
-                if not second:
-                    sums = [bank(HALVES * pair + m, PAIR) for m in range(HALVES)]
-                for m in range(HALVES):
-                    multiply(sums[m][:, CHUNK * second : CHUNK * (second + 1)], m, c, 1)
-            elif pair < last_pair:
-                if not second:
-                    sums = [bank(HALVES * pair + m, PAIR) for m in range(HALVES)]
-                multiply(sums[0][:, CHUNK * second : CHUNK * (second + 1)], 0, c, 1)
-                if second:
-                    multiply(sums[1], 1, c - 1, 2)
+            gather_pairs(3, 2 + c, 1, later[c])
+            for m in range(HALVES):
+                multiply(chunk_of(sums[0], m, c), m, c, 1)
 
+        interleave_on_scalar(PAIR, 2 * PAIR, range(home(1, 1), home(3, 1) + 1, PAIRS))
+        empty(0, sums[0])
+        for c in (2, 3):
+            quantize(c)
+            for m in range(HALVES):
+                multiply(chunk_of(sums[1], m, c), m, c, 1)
+        gather_pairs(2, 3, 1, last_strips[1])
+
+        interleave_on_scalar(2 * PAIR, 3 * PAIR, range(home(2, 2), home(3, 2) + 1, PAIRS))
+        empty(1, sums[1])
+        for c in (4, 5):
+            quantize(c)
+            multiply(chunk_of(sums[2], 0, c), 0, c, 1)
+        multiply(sums[2][1], 1, 4, 2)
+
+        for c in (6, 7):
+            interleave_on_vector(CHUNK * c, CHUNK * (c + 1), last_strips)
+        empty(2, sums[2])
+        for c in (6, 7):
+            quantize(c)
+
+        last_pair = PAIRS - 1
         for m, (copy, banks) in enumerate(((on_vector, (6, 7)), (on_scalar, (0, 1)))):
             for c, b in enumerate(banks):
                 acc = bank(b, CHUNK)

@@ -20,10 +20,11 @@ PACK = 4
 HALVES = M // P
 CHUNK = 128
 CHUNKS = S // CHUNK
-PAIR = 2 * CHUNK
-PAIRS = S // PAIR
 
-EARLY_PAIRS = 3
+GROUPS = ((0, 1), (2, 3), (4, 5), (6, 7))
+EARLY_CHUNKS = 6
+PAIRED_CHUNKS = 5
+WARM_M, WARM_N, WARM_PASSES = 32, 512, 2
 
 KIB = 1024
 ZONE = 32 * KIB
@@ -64,24 +65,25 @@ def tile_list_heads_none_kernel(
         spread = place("spread", [P, S], F32, 4, WEIGHT_ZONE)
         planes = [place(f"plane{i}", [P, T], F32, 4, PLANE_ZONES[i % 2]) for i in range(PACK)]
         w4 = place("w4", [P, 2 * M], U8, 1, EARLY_ZONE)
-        r8 = place("r8", [P, M], U32, 4, EARLY_ZONE)
+        r8 = place("r8", [P, WARM_N], U32, 4, EARLY_ZONE)
         w4s = place("w4s", [P, M], U8, 1, EARLY_ZONE)
-        r8s = place("r8s", [P, M], U8, 1, EARLY_ZONE)
+        r8s = place("r8s", [P, WARM_N], U8, 1, EARLY_ZONE)
         picked_at = LATE_ZONE * ZONE - RESERVED - 2 * S * 4
-        picked = keep.tile([P, PACK * PAIRS, PAIR], F32, name="picked", align_bytes=KIB, offset=picked_at)
+        picked = keep.tile([P, 30, CHUNK], F32, name="picked", align_bytes=KIB, offset=picked_at)
         woven = place("woven", [P, S, PACK], BF16, 2, WOVEN_ZONE)
         codes = place("codes", [P, S], U32, 4, CODES_ZONE)
         scales = place("scales", [P, S], U8, 1, CODES_ZONE)
         results = [
-            place(f"result{n}", [P, PAIR], F32, 4, RESULT_ZONES[n % len(RESULT_ZONES)])
-            for n in range(HALVES * CHUNKS // 2)
+            place(f"result{n}", [P, CHUNK * len(GROUPS[n // 2])], F32, 4, RESULT_ZONES[n % len(RESULT_ZONES)])
+            for n in range(HALVES * len(GROUPS))
         ]
 
         nc.vector.memset(r8s[:].bitcast(I32), 0)
         nc.vector.memset(w4s[:].bitcast(I32), 0)
+        nc.vector.memset(r8[:, M:WARM_N], 0)
 
         def load_scales(tile, src, q):
-            nc.sync.dma_start(tile[32 * q : 32 * q + 4, :].bitcast(I32), src[0, 4 * q : 4 * q + 4, :].bitcast(I32))
+            nc.sync.dma_start(tile[32 * q : 32 * q + 4, 0:M].bitcast(I32), src[0, 4 * q : 4 * q + 4, :].bitcast(I32))
 
         nc.sync.dma_start(rows[:], wgt.rearrange("p (h e) -> (p h) e", e=512)[0:256:17])
         nc.sync.dma_start(planes[0][:], plane_rows[0])
@@ -90,8 +92,8 @@ def tile_list_heads_none_kernel(
             nc.sync.dma_start(planes[i][:], plane_rows[i])
             for q in quadrants:
                 load_scales(r8s, r8_scales, q)
+        nc.sync.dma_start(r8[:, 0:M].bitcast(I32), r8_words[0].rearrange("p n t -> p (n t)").bitcast(I32))
         nc.sync.dma_start(w4[:].bitcast(I32), w4_words[0].bitcast(I32))
-        nc.sync.dma_start(r8[:].bitcast(I32), r8_words[0].rearrange("p n t -> p (n t)").bitcast(I32))
         for q in range(4):
             load_scales(w4s, w4_scales, q)
 
@@ -106,52 +108,52 @@ def tile_list_heads_none_kernel(
         for a in (0, 512):
             nc.vector.transpose(weight[:, a : a + 512], spread[:, a : a + 512])
 
-        def gather(dst, i, a, b):
-            nc.vector.tensor_tensor(dst, planes[i][:].indirect(offsets[:, a // 16 : b // 16]), weight[:, a:b], MULT)
-
-        def home(i, pair):
-            return PAIRS * i + pair
-
-        def gather_pairs(i, first, n, at):
-            gather(picked[:, at : at + n, :].rearrange("p r n -> p (r n)"), i, PAIR * first, PAIR * (first + n))
-
-        def xb(a, b):
-            return woven[:, a:b, :]
-
-        def late_planes(a, b, strips):
-            at = a % PAIR
-            return PACK - len(strips), picked[:, strips.start : strips.stop : strips.step, at : at + b - a]
-
-        def interleave_on_scalar(a, b, strips):
-            i, values = late_planes(a, b, strips)
-            on_scalar(xb(a, b)[:, :, i:PACK], values.rearrange("p t n -> p n t"))
-
-        def interleave_on_vector(a, b, strips):
-            i, values = late_planes(a, b, strips)
-            on_vector(
-                xb(a, b)[:, :, i:PACK].rearrange("p (c n) t -> p c t n", n=2),
-                values.rearrange("p t (c n) -> p c t n", n=2),
+        def gather(i, first, n, strip):
+            a, b = CHUNK * first, CHUNK * (first + n)
+            nc.vector.tensor_tensor(
+                picked[:, strip : strip + n, :].rearrange("p r n -> p (r n)"),
+                planes[i][:].indirect(offsets[:, a // 16 : b // 16]),
+                weight[:, a:b],
+                MULT,
             )
 
-        by_pair = woven[:].rearrange("p (r n) t -> p r n t", n=PAIR)
-        gather_pairs(0, 0, PAIRS, home(0, 0))
-        on_scalar(by_pair[:, 1:PAIRS:2, :, 0], picked[:, 1:PAIRS:2, :])
-        gather_pairs(1, 0, PAIRS, home(1, 0))
-        on_scalar(
-            by_pair[:, 0:PAIRS:2, :, 0:2].rearrange("p r (c n) t -> p r c t n", n=4),
-            picked[:, 0 : 2 * PAIRS : 2, :].rearrange("p (t r) (c n) -> p r c t n", t=2, n=4),
-        )
+        def xb(first, n=1):
+            return woven[:, CHUNK * first : CHUNK * (first + n), :]
+
+        late = {
+            0: range(16, 29, 12),
+            1: range(17, 26, 8),
+            2: range(18, 24, 5),
+            3: range(19, 25, 5),
+            4: range(20, 29, 8),
+            5: range(13, 30, 8),
+            6: range(14, 23, 4),
+            7: range(15, 24, 4),
+        }
+
+        def late_values(c):
+            strips = late[c]
+            return PACK - len(strips), picked[:, strips.start : strips.stop : strips.step, :]
+
+        def interleave_on_scalar(c):
+            i, values = late_values(c)
+            on_scalar(xb(c)[:, :, i:PACK], values.rearrange("p t n -> p n t"))
+
+        def interleave_on_vector(c):
+            i, values = late_values(c)
+            on_vector(
+                xb(c)[:, :, i:PACK].rearrange("p (c n) t -> p c t n", n=2),
+                values.rearrange("p t (c n) -> p c t n", n=2),
+            )
 
         def quantize(c):
             cols = slice(CHUNK * c, CHUNK * (c + 1))
             nc.vector.quantize_mx(
-                out=codes[:, cols].bitcast(FP8X4),
-                scales=scales[:, cols],
-                in_=xb(cols.start, cols.stop).rearrange("p n t -> p (n t)"),
+                out=codes[:, cols].bitcast(FP8X4), scales=scales[:, cols], in_=xb(c).rearrange("p n t -> p (n t)")
             )
 
-        def multiply(acc, m, first, n):
-            cols = slice(CHUNK * first, CHUNK * (first + n))
+        def multiply(acc, m, c, n=1):
+            cols = slice(CHUNK * c, CHUNK * (c + n))
             stationary = (
                 (w4[:, 2 * P * m : 2 * P * (m + 1)].bitcast(FP4X4), w4s),
                 (r8[:, P * m : P * (m + 1)].bitcast(FP8X4), r8s),
@@ -170,56 +172,72 @@ def tile_list_heads_none_kernel(
         def bank(b, width):
             return psum.tile([P, width], F32, name=f"bank{b}")[:]
 
-        def store(pair, m):
-            nc.sync.dma_start(out_halves[:, m, PAIR * pair : PAIR * (pair + 1)], results[HALVES * pair + m][:])
+        def store(g, m):
+            a = CHUNK * GROUPS[g][0]
+            nc.sync.dma_start(out_halves[:, m, a : a + CHUNK * len(GROUPS[g])], results[HALVES * g + m][:])
 
-        def empty(pair, sums):
+        def empty(g):
             for m in range(HALVES):
-                on_scalar(results[HALVES * pair + m][:], sums[m])
-                store(pair, m)
+                on_scalar(results[HALVES * g + m][:], sums[g][m])
+                store(g, m)
 
-        def chunk_of(sums, m, c):
-            return sums[m][:, CHUNK * (c % 2) : CHUNK * (c % 2 + 1)]
-
-        sums = [[bank(HALVES * pair + m, PAIR) for m in range(HALVES)] for pair in range(PAIRS - 1)]
-        gather_pairs(2, 0, EARLY_PAIRS, home(2, 0))
-        last_strips = range(home(1, 3), home(2, 3) + 1, 2)
-        later = (home(3, 2), last_strips[2])
-        for c in range(2):
-            gather(picked[:, later[c], CHUNK * c : CHUNK * (c + 1)], 3, CHUNK * c, CHUNK * (c + 1))
-        gather_pairs(3, 1, 1, home(3, 1))
-        for c in range(2):
-            interleave_on_scalar(CHUNK * c, CHUNK * (c + 1), range(home(2, 0), later[c] + 1, later[c] - home(2, 0)))
+        def quantize_and_multiply(c):
             quantize(c)
-            gather_pairs(3, 2 + c, 1, later[c])
+            g, at = divmod(c, 2)
             for m in range(HALVES):
-                multiply(chunk_of(sums[0], m, c), m, c, 1)
+                multiply(sums[g][m][:, CHUNK * at : CHUNK * (at + 1)], m, c)
 
-        interleave_on_scalar(PAIR, 2 * PAIR, range(home(1, 1), home(3, 1) + 1, PAIRS))
-        empty(0, sums[0])
-        for c in (2, 3):
-            quantize(c)
-            for m in range(HALVES):
-                multiply(chunk_of(sums[1], m, c), m, c, 1)
-        gather_pairs(2, 3, 1, last_strips[1])
+        flat = picked[:].rearrange("p r n -> p (r n)")
+        cut = CHUNK * PAIRED_CHUNKS
+        gather(0, 0, CHUNKS, 0)
+        on_scalar(woven[:, cut:S, 0], flat[:, cut:S])
+        gather(1, 0, CHUNKS, CHUNKS)
+        on_scalar(
+            woven[:, 0:cut, 0:2].rearrange("p (c n) t -> p c t n", n=4),
+            flat[:, 0 : 2 * S].rearrange("p (t j) -> p t j", t=2)[:, :, 0:cut].rearrange("p t (c n) -> p c t n", n=4),
+        )
+        gather(2, 0, EARLY_CHUNKS, 2 * CHUNKS)
 
-        interleave_on_scalar(2 * PAIR, 3 * PAIR, range(home(2, 2), home(3, 2) + 1, PAIRS))
-        empty(1, sums[1])
+        idle = psum.tile([WARM_M, WARM_N], F32, name="bank7")
+        for n in range(WARM_PASSES):
+            nc.tensor.matmul_mx(
+                out=idle[:],
+                lhsT=r8[:, 0:WARM_M].bitcast(FP8X4),
+                lhsT_scale=r8s[:, 0:WARM_M],
+                rhs=r8[:].bitcast(FP8X4),
+                rhs_scale=r8s[:],
+                start=True,
+                stop=True,
+            )
+
+        sums = [[bank(HALVES * g + m, 2 * CHUNK) for m in range(HALVES)] for g in range(3)]
+        gather(3, 0, 1, late[0][-1])
+        gather(3, 1, 1, late[1][-1])
+        gather(3, 2, 2, late[2][-1])
+        interleave_on_scalar(0)
+        quantize_and_multiply(0)
+        gather(3, 4, 2, late[4][-1])
+        for c in (1, 2):
+            interleave_on_scalar(c)
+            quantize_and_multiply(c)
+        gather(3, 6, 2, late[6][-1])
+        interleave_on_scalar(3)
+        quantize_and_multiply(3)
+        gather(2, 6, 2, late[6][1])
         for c in (4, 5):
+            interleave_on_scalar(c)
             quantize(c)
-            multiply(chunk_of(sums[2], 0, c), 0, c, 1)
+            multiply(sums[2][0][:, CHUNK * (c - 4) : CHUNK * (c - 3)], 0, c)
         multiply(sums[2][1], 1, 4, 2)
-
-        for c in (6, 7):
-            interleave_on_vector(CHUNK * c, CHUNK * (c + 1), last_strips)
-        empty(2, sums[2])
-        for c in (6, 7):
+        for g in range(3):
+            empty(g)
+        for c in GROUPS[3]:
+            interleave_on_vector(c)
+        for c in GROUPS[3]:
             quantize(c)
-
-        last_pair = PAIRS - 1
         for m, (copy, banks) in enumerate(((on_vector, (6, 7)), (on_scalar, (0, 1)))):
-            for c, b in enumerate(banks):
+            for at, b in enumerate(banks):
                 acc = bank(b, CHUNK)
-                multiply(acc, m, 2 * last_pair + c, 1)
-                copy(results[HALVES * last_pair + m][:, CHUNK * c : CHUNK * (c + 1)], acc)
-            store(last_pair, m)
+                multiply(acc, m, GROUPS[3][at])
+                copy(results[HALVES * 3 + m][:, CHUNK * at : CHUNK * (at + 1)], acc)
+            store(3, m)

@@ -198,7 +198,7 @@ def tile_list_heads_none_kernel(
         )
         gather(2, 0, EARLY_CHUNKS, 2 * CHUNKS)
 
-        idle = psum.tile([WARM_M, WARM_N], F32, name="bank7")
+        idle = psum.tile([WARM_M, WARM_N], F32, name="bank0")
         for n in range(WARM_PASSES):
             nc.tensor.matmul_mx(
                 out=idle[:],
@@ -210,7 +210,9 @@ def tile_list_heads_none_kernel(
                 stop=True,
             )
 
-        sums = [[bank(HALVES * g + m, 2 * CHUNK) for m in range(HALVES)] for g in range(3)]
+        shared = [bank(g, 4 * CHUNK) for g in range(2)]
+        sums = [[both[:, 2 * CHUNK * m : 2 * CHUNK * (m + 1)] for m in range(HALVES)] for both in shared]
+        sums.append([bank(2 + m, 2 * CHUNK) for m in range(HALVES)])
         gather(3, 0, 1, late[0][-1])
         gather(3, 1, 1, late[1][-1])
         gather(3, 2, 2, late[2][-1])
@@ -235,7 +237,7 @@ def tile_list_heads_none_kernel(
             interleave_on_vector(c)
         for c in GROUPS[3]:
             quantize(c)
-        for m, (copy, banks) in enumerate(((on_vector, (6, 7)), (on_scalar, (0, 1)))):
+        for m, (copy, banks) in enumerate(((on_vector, (4, 5)), (on_scalar, (6, 7)))):
             for at, b in enumerate(banks):
                 acc = bank(b, CHUNK)
                 multiply(acc, m, GROUPS[3][at])

@@ -22,7 +22,7 @@ CHUNK = 128
 CHUNKS = S // CHUNK
 
 GROUPS = ((0, 1), (2, 3), (4, 5), (6, 7))
-EARLY_CHUNKS = 6
+EARLY = 832
 PAIRED_CHUNKS = 5
 WARM_M, WARM_N, WARM_PASSES = 32, 512, 2
 
@@ -69,7 +69,7 @@ def tile_list_heads_none_kernel(
         w4s = place("w4s", [P, M], U8, 1, EARLY_ZONE)
         r8s = place("r8s", [P, WARM_N], U8, 1, EARLY_ZONE)
         picked_at = LATE_ZONE * ZONE - RESERVED - 2 * S * 4
-        picked = keep.tile([P, 30, CHUNK], F32, name="picked", align_bytes=KIB, offset=picked_at)
+        picked = keep.tile([P, 32, CHUNK], F32, name="picked", align_bytes=KIB, offset=picked_at)
         woven = place("woven", [P, S, PACK], BF16, 2, WOVEN_ZONE)
         codes = place("codes", [P, S], U32, 4, CODES_ZONE)
         scales = place("scales", [P, S], U8, 1, CODES_ZONE)
@@ -123,12 +123,12 @@ def tile_list_heads_none_kernel(
         late = {
             0: range(16, 29, 12),
             1: range(17, 26, 8),
-            2: range(18, 24, 5),
-            3: range(19, 25, 5),
+            2: range(18, 32, 13),
+            3: range(19, 24, 4),
             4: range(20, 29, 8),
             5: range(13, 30, 8),
-            6: range(14, 23, 4),
-            7: range(15, 24, 4),
+            6: range(14, 31, 8),
+            7: range(15, 32, 8),
         }
 
         def late_values(c):
@@ -196,7 +196,13 @@ def tile_list_heads_none_kernel(
             woven[:, 0:cut, 0:2].rearrange("p (c n) t -> p c t n", n=4),
             flat[:, 0 : 2 * S].rearrange("p (t j) -> p t j", t=2)[:, :, 0:cut].rearrange("p t (c n) -> p c t n", n=4),
         )
-        gather(2, 0, EARLY_CHUNKS, 2 * CHUNKS)
+
+        def gather_plane_2(a, b):
+            nc.vector.tensor_tensor(
+                flat[:, 2 * S + a : 2 * S + b], planes[2][:].indirect(offsets[:, a // 16 : b // 16]), weight[:, a:b], MULT
+            )
+
+        gather_plane_2(0, EARLY)
 
         idle = psum.tile([WARM_M, WARM_N], F32, name="bank0")
         for n in range(WARM_PASSES):
@@ -213,9 +219,8 @@ def tile_list_heads_none_kernel(
         shared = [bank(g, 4 * CHUNK) for g in range(2)]
         sums = [[both[:, 2 * CHUNK * m : 2 * CHUNK * (m + 1)] for m in range(HALVES)] for both in shared]
         sums.append([bank(2 + m, 2 * CHUNK) for m in range(HALVES)])
-        gather(3, 0, 1, late[0][-1])
-        gather(3, 1, 1, late[1][-1])
-        gather(3, 2, 2, late[2][-1])
+        for c in range(4):
+            gather(3, c, 1, late[c][-1])
         interleave_on_scalar(0)
         quantize_and_multiply(0)
         gather(3, 4, 2, late[4][-1])
@@ -225,7 +230,7 @@ def tile_list_heads_none_kernel(
         gather(3, 6, 2, late[6][-1])
         interleave_on_scalar(3)
         quantize_and_multiply(3)
-        gather(2, 6, 2, late[6][1])
+        gather_plane_2(EARLY, S)
         for c in (4, 5):
             interleave_on_scalar(c)
             quantize(c)

@@ -131,20 +131,18 @@ def tile_list_heads_none_kernel(
             7: range(15, 32, 8),
         }
 
-        def late_values(c):
+        def late_values(c, a, b):
             strips = late[c]
-            return PACK - len(strips), picked[:, strips.start : strips.stop : strips.step, :]
+            i = PACK - len(strips)
+            return xb(c)[:, a:b, i:PACK], picked[:, strips.start : strips.stop : strips.step, a:b]
 
-        def interleave_on_scalar(c):
-            i, values = late_values(c)
-            on_scalar(xb(c)[:, :, i:PACK], values.rearrange("p t n -> p n t"))
+        def interleave_on_scalar(c, a=0, b=CHUNK):
+            dst, values = late_values(c, a, b)
+            on_scalar(dst, values.rearrange("p t n -> p n t"))
 
-        def interleave_on_vector(c):
-            i, values = late_values(c)
-            on_vector(
-                xb(c)[:, :, i:PACK].rearrange("p (c n) t -> p c t n", n=2),
-                values.rearrange("p t (c n) -> p c t n", n=2),
-            )
+        def interleave_on_vector(c, a=0, b=CHUNK):
+            dst, values = late_values(c, a, b)
+            on_vector(dst.rearrange("p (c n) t -> p c t n", n=2), values.rearrange("p t (c n) -> p c t n", n=2))
 
         def quantize(c):
             cols = slice(CHUNK * c, CHUNK * (c + 1))
@@ -236,12 +234,17 @@ def tile_list_heads_none_kernel(
             quantize(c)
             multiply(sums[2][0][:, CHUNK * (c - 4) : CHUNK * (c - 3)], 0, c)
         multiply(sums[2][1], 1, 4, 2)
-        for g in range(3):
+        share = EARLY - CHUNK * 6
+        interleave_on_scalar(6, 0, share)
+        for g in range(2):
             empty(g)
-        for c in GROUPS[3]:
-            interleave_on_vector(c)
+        interleave_on_vector(6, share, CHUNK)
+        interleave_on_vector(7)
         for c in GROUPS[3]:
             quantize(c)
+        for m, copy in enumerate((on_vector, on_scalar)):
+            copy(results[HALVES * 2 + m][:], sums[2][m])
+            store(2, m)
         for m, (copy, banks) in enumerate(((on_vector, (4, 5)), (on_scalar, (6, 7)))):
             for at, b in enumerate(banks):
                 acc = bank(b, CHUNK)

from contextlib import ExitStack

import concourse.mybir as mybir

K, M, T, S = 512, 256, 2048, 1024
FLOPS = 2 * 2 * K * M * S

F32 = mybir.dt.float32
BF16 = mybir.dt.bfloat16
I32 = mybir.dt.int32
U32 = mybir.dt.uint32
U16 = mybir.dt.uint16
U8 = mybir.dt.uint8
FP8X4 = mybir.dt.float8_e4m3fn_x4
FP4X4 = mybir.dt.float4_e2m1fn_x4
MULT = mybir.AluOpType.mult

P = 128
PACK = 4
HALVES = M // P
CHUNK = 128
CHUNKS = S // CHUNK

GROUPS = ((0, 1), (2, 3), (4, 5), (6, 7))
EARLY = 832
PAIRED_CHUNKS = 5
WARM_M, WARM_N, WARM_PASSES = 32, 512, 2

KIB = 1024
ZONE = 32 * KIB
RESERVED = 17 * KIB
WEIGHT_ZONE, EARLY_ZONE, LATE_ZONE, WOVEN_ZONE, CODES_ZONE, SPARE_ZONE = 0, 3, 4, 5, 6, 7
PLANE_ZONES = (1, 2)
RESULT_ZONES = (SPARE_ZONE, EARLY_ZONE, PLANE_ZONES[1], PLANE_ZONES[0])


def tile_list_heads_none_kernel(
    tc, xT, w4_words, w4_scales, r8_words, r8_scales, wgt, offs, out
):
    nc = tc.nc
    plane_rows = xT.rearrange("(p i) t -> i p t", i=PACK)
    out_halves = out.rearrange("(m p) j -> p m j", p=P)
    on_scalar, on_vector = nc.scalar.copy, nc.vector.tensor_copy

    with ExitStack() as ctx:
        keep = ctx.enter_context(tc.tile_pool(name="keep", bufs=1))
        lists = ctx.enter_context(tc.tile_pool(name="lists", bufs=1))
        psum = ctx.enter_context(tc.psum_pool(name="psum", bufs=1))

        filled = {}

        def place(name, shape, dtype, itemsize, zone):
            used = filled.get(zone, 0)
            size = itemsize
            for n in shape[1:]:
                size = size * n
            filled[zone] = used + (size + KIB - 1) // KIB * KIB
            start = max(zone * ZONE - RESERVED, 0)
            return keep.tile(shape, dtype, name=name, align_bytes=KIB, offset=start + used)

        offsets = lists.tile([P, S // 16], U16, name="offsets")
        weight = place("weight", [P, S], F32, 4, WEIGHT_ZONE)
        rows = place("rows", [P, 64], F32, 4, WEIGHT_ZONE)
        turned = place("turned", [P, 64], F32, 4, WEIGHT_ZONE)
        spread = place("spread", [P, S], F32, 4, WEIGHT_ZONE)
        planes = [place(f"plane{i}", [P, T], F32, 4, PLANE_ZONES[i % 2]) for i in range(PACK)]
        w4 = place("w4", [P, 2 * M], U8, 1, EARLY_ZONE)
        r8 = place("r8", [P, WARM_N], U32, 4, EARLY_ZONE)
        w4s = place("w4s", [P, M], U8, 1, EARLY_ZONE)
        r8s = place("r8s", [P, WARM_N], U8, 1, EARLY_ZONE)
        picked_at = LATE_ZONE * ZONE - RESERVED - 2 * S * 4
        picked = keep.tile([P, 32, CHUNK], F32, name="picked", align_bytes=KIB, offset=picked_at)
        woven = place("woven", [P, S, PACK], BF16, 2, WOVEN_ZONE)
        codes = place("codes", [P, S], U32, 4, CODES_ZONE)
        scales = place("scales", [P, S], U8, 1, CODES_ZONE)
        results = [
            place(f"result{n}", [P, CHUNK * len(GROUPS[n // 2])], F32, 4, RESULT_ZONES[n % len(RESULT_ZONES)])
            for n in range(HALVES * len(GROUPS))
        ]

        nc.vector.memset(r8s[:].bitcast(I32), 0)
        nc.vector.memset(w4s[:].bitcast(I32), 0)
        nc.vector.memset(r8[:, M:WARM_N], 0)

        def load_scales(tile, src, q):
            nc.sync.dma_start(tile[32 * q : 32 * q + 4, 0:M].bitcast(I32), src[0, 4 * q : 4 * q + 4, :].bitcast(I32))

        nc.sync.dma_start(rows[:], wgt.rearrange("p (h e) -> (p h) e", e=512)[0:256:17])
        nc.sync.dma_start(planes[0][:], plane_rows[0])
        nc.sync.dma_start(offsets[:], offs)
        for i, quadrants in ((1, (0, 1)), (2, (2,)), (3, (3,))):
            nc.sync.dma_start(planes[i][:], plane_rows[i])
            for q in quadrants:
                load_scales(r8s, r8_scales, q)
        nc.sync.dma_start(r8[:, 0:M].bitcast(I32), r8_words[0].rearrange("p n t -> p (n t)").bitcast(I32))
        nc.sync.dma_start(w4[:].bitcast(I32), w4_words[0].bitcast(I32))
        for q in range(4):
            load_scales(w4s, w4_scales, q)

        for a in (0, 32):
            nc.vector.transpose(turned[:, a : a + 32], rows[:, a : a + 32])
        by_block = turned[:].rearrange("p (g b) -> p b g", b=16)
        for a, copy in ((0, on_vector), (512, on_scalar)):
            copy(
                spread[:, a : a + 512].rearrange("p (b g r) -> p b g r", g=4, r=16),
                by_block[:, a // 64 : a // 64 + 8, :].unsqueeze(3).broadcast_to([P, 8, 4, 16]),
            )
        for a in (0, 512):
            nc.vector.transpose(weight[:, a : a + 512], spread[:, a : a + 512])

        def gather(i, first, n, strip):
            a, b = CHUNK * first, CHUNK * (first + n)
            nc.vector.tensor_tensor(
                picked[:, strip : strip + n, :].rearrange("p r n -> p (r n)"),
                planes[i][:].indirect(offsets[:, a // 16 : b // 16]),
                weight[:, a:b],
                MULT,
            )

        def xb(first, n=1):
            return woven[:, CHUNK * first : CHUNK * (first + n), :]

        late = {
            0: range(16, 29, 12),
            1: range(17, 26, 8),
            2: range(18, 32, 13),
            3: range(19, 24, 4),
            4: range(20, 29, 8),
            5: range(13, 30, 8),
            6: range(14, 31, 8),
            7: range(15, 32, 8),
        }

        def late_values(c, a, b):
            strips = late[c]
            i = PACK - len(strips)
            return xb(c)[:, a:b, i:PACK], picked[:, strips.start : strips.stop : strips.step, a:b]

        def interleave_on_scalar(c, a=0, b=CHUNK):
            dst, values = late_values(c, a, b)
            on_scalar(dst, values.rearrange("p t n -> p n t"))

        def interleave_on_vector(c, a=0, b=CHUNK):
            dst, values = late_values(c, a, b)
            on_vector(dst.rearrange("p (c n) t -> p c t n", n=2), values.rearrange("p t (c n) -> p c t n", n=2))

        def quantize(c):
            cols = slice(CHUNK * c, CHUNK * (c + 1))
            nc.vector.quantize_mx(
                out=codes[:, cols].bitcast(FP8X4), scales=scales[:, cols], in_=xb(c).rearrange("p n t -> p (n t)")
            )

        def multiply(acc, m, c, n=1):
            cols = slice(CHUNK * c, CHUNK * (c + n))
            stationary = (
                (w4[:, 2 * P * m : 2 * P * (m + 1)].bitcast(FP4X4), w4s),
                (r8[:, P * m : P * (m + 1)].bitcast(FP8X4), r8s),
            )
            for t, (words, plane) in enumerate(stationary):
                nc.tensor.matmul_mx(
                    out=acc,
                    lhsT=words,
                    lhsT_scale=plane[:, P * m : P * (m + 1)],
                    rhs=codes[:, cols].bitcast(FP8X4),
                    rhs_scale=scales[:, cols],
                    start=t == 0,
                    stop=t == 1,
                )

        def bank(b, width):
            return psum.tile([P, width], F32, name=f"bank{b}")[:]

        def store(g, m):
            a = CHUNK * GROUPS[g][0]
            nc.sync.dma_start(out_halves[:, m, a : a + CHUNK * len(GROUPS[g])], results[HALVES * g + m][:])

        def empty(g):
            for m in range(HALVES):
                on_scalar(results[HALVES * g + m][:], sums[g][m])
                store(g, m)

        def quantize_and_multiply(c):
            quantize(c)
            g, at = divmod(c, 2)
            for m in range(HALVES):
                multiply(sums[g][m][:, CHUNK * at : CHUNK * (at + 1)], m, c)

        flat = picked[:].rearrange("p r n -> p (r n)")
        cut = CHUNK * PAIRED_CHUNKS
        gather(0, 0, CHUNKS, 0)
        on_scalar(woven[:, cut:S, 0], flat[:, cut:S])
        gather(1, 0, CHUNKS, CHUNKS)
        on_scalar(
            woven[:, 0:cut, 0:2].rearrange("p (c n) t -> p c t n", n=4),
            flat[:, 0 : 2 * S].rearrange("p (t j) -> p t j", t=2)[:, :, 0:cut].rearrange("p t (c n) -> p c t n", n=4),
        )

        def gather_plane_2(a, b):
            nc.vector.tensor_tensor(
                flat[:, 2 * S + a : 2 * S + b], planes[2][:].indirect(offsets[:, a // 16 : b // 16]), weight[:, a:b], MULT
            )

        gather_plane_2(0, EARLY)

        idle = psum.tile([WARM_M, WARM_N], F32, name="bank0")
        for n in range(WARM_PASSES):
            nc.tensor.matmul_mx(
                out=idle[:],
                lhsT=r8[:, 0:WARM_M].bitcast(FP8X4),
                lhsT_scale=r8s[:, 0:WARM_M],
                rhs=r8[:].bitcast(FP8X4),
                rhs_scale=r8s[:],
                start=True,
                stop=True,
            )

        shared = [bank(g, 4 * CHUNK) for g in range(2)]
        sums = [[both[:, 2 * CHUNK * m : 2 * CHUNK * (m + 1)] for m in range(HALVES)] for both in shared]
        sums.append([bank(2 + m, 2 * CHUNK) for m in range(HALVES)])
        for c in range(4):
            gather(3, c, 1, late[c][-1])
        interleave_on_scalar(0)
        quantize_and_multiply(0)
        gather(3, 4, 2, late[4][-1])
        for c in (1, 2):
            interleave_on_scalar(c)
            quantize_and_multiply(c)
        gather(3, 6, 2, late[6][-1])
        interleave_on_scalar(3)
        quantize_and_multiply(3)
        gather_plane_2(EARLY, S)
        for c in (4, 5):
            interleave_on_scalar(c)
            quantize(c)
            multiply(sums[2][0][:, CHUNK * (c - 4) : CHUNK * (c - 3)], 0, c)
        multiply(sums[2][1], 1, 4, 2)
        share = EARLY - CHUNK * 6
        interleave_on_scalar(6, 0, share)
        for g in range(2):
            empty(g)
        interleave_on_vector(6, share, CHUNK)
        interleave_on_vector(7)
        for c in GROUPS[3]:
            quantize(c)
        for m, copy in enumerate((on_vector, on_scalar)):
            copy(results[HALVES * 2 + m][:], sums[2][m])
            store(2, m)
        for m, (copy, banks) in enumerate(((on_vector, (4, 5)), (on_scalar, (6, 7)))):
            for at, b in enumerate(banks):
                acc = bank(b, CHUNK)
                multiply(acc, m, GROUPS[3][at])
                copy(results[HALVES * 3 + m][:, CHUNK * at : CHUNK * (at + 1)], acc)
            store(3, m)
